import numpy as np, ml_dtypes
CORES = [1,5,17,21,33,37,49,53]
N = 8
BF = ml_dtypes.bfloat16
def gentries(a):
    return np.ascontiguousarray(a.reshape(8, 16, -1).transpose(0, 2, 1)).reshape(8, -1)
def gtable(e):
    e = np.asarray(e); return np.ascontiguousarray(e.reshape(8, -1, 16).transpose(0, 2, 1)).reshape(128, -1).astype(np.int32)
W, L, U, T, A, K, Q = 2048, 160, 96, 6, 2, 960, 960
def pack(x, b, o, w, t):
    return {"xs": np.ascontiguousarray(x.reshape(N, 128, W)).astype(np.float32).astype(BF), "nb": np.ascontiguousarray(b.reshape(N, 128, W)).astype(np.int32),
            "od": np.stack([gtable(a) for a in o]), "wt": np.ascontiguousarray(w.reshape(N, 128, 1)).astype(np.int32), "th": np.ascontiguousarray(t.reshape(N, 8, 1)).astype(np.int32)}
def parts(rng):
    amp = 4 + 86 * rng.random((N, 8, 1, W)); mid = rng.integers(96, 160, (1, 8, 16, 1))
    x = np.clip(np.rint(mid + amp * rng.standard_normal((N, 8, 16, W), dtype=np.float32)), 0, 255).astype(np.int64)
    b = rng.integers(0, W, (N, 8, 16, W)); o = np.argsort(rng.random((N, 8, W)), axis=-1)[..., :Q]
    return x, b, o, rng.integers(0, 256, (N, 8, 16)), rng.integers(300, 1000, (N, 8))
def setup_inputs(rng):
    return pack(*parts(rng))
def setup_inputs_spread(rng):
    x, b, o, w, t = parts(rng)
    x = np.floor(np.exp2(8 * rng.random((N, 8, 1, W))) * rng.random((N, 8, 16, W))).astype(np.int64)
    b = np.floor(W * rng.random((N, 8, 16, W)) ** 3).astype(np.int64)
    w = np.floor(np.exp2(8 * rng.random((N, 8, 16))) - 1).astype(np.int64); t = np.floor(np.exp2(12 * rng.random((N, 8))) - 1).astype(np.int64)
    x[:, 6] = rng.integers(192, 256, (N, 16, W)); w[:, 6] = rng.integers(240, 256, (N, 16)); t[:, 6] = 0
    return pack(x, b, o, w, t)
def setup_inputs_ends(rng):
    lo = rng.integers(0, 2, 8) * 255; lo[7] = 0; base = lo.reshape(1, 8, 1, 1)
    u = rng.random((N, 8, 1, W)); e = 255 * rng.integers(0, 2, (N, 8, 16, W))
    x = np.where(u < 0.5, 255 - base, np.where(u < 0.7, base, e))
    x[..., [0, W - 1]] = base; x[:, ::2, :, 1] = lo[::2].reshape(1, 4, 1); x[:, 7, :, 1:8] = 0; x[:, 7, 15, W - 1] = 255
    b = (W - 1) * rng.integers(0, 2, (N, 8, 16, W))
    b = np.where(rng.random((N, 8, 1, W)) < 0.2, (W - 1) * rng.integers(0, 2, (N, 8, 1, W)), b)
    for step in range(A, T):
        place = (16 * 255 * 255 + 77 * step) & (W - 1)
        b[:, 7, :, place] = 0; b[1::2, 7, 15, place] = W - 1; b[:, 7, 5, (77 * step) & (W - 1)] = W - 1
    s = np.zeros(Q, np.int64); h = Q // 2; s[0::2] = np.arange(Q - h); s[1::2] = W - 1 - np.arange(h)
    key = rng.random((N, 8, T, L)); key[:, :, 0, 0] = -3; key[:, :, 0, 1] = -2; key[:, :, 0, 2] = -1
    o = s.reshape(T, L)[np.arange(T)[:, None], np.argsort(key, axis=-1)].reshape(N, 8, Q)
    for q in range(N):
        x[q, 7][:, o[q, 7][np.array([3, 4, U - 2, U - 1, L - 2, L - 1])]] = 255
    kd = rng.integers(0, 3, (N, 8, 1)); w = np.where(kd == 0, 255, np.where(kd == 1, 0, 255 * rng.integers(0, 2, (N, 8, 16))))
    w[:, 7] = 255; w[:, 0, ::2] = 0; w[:, 0, 1::2] = 255
    t = 4095 * (rng.random((N, 8)) < 0.3).astype(np.int64)
    for q in range(N): t[q, q % 7] = 4095
    t[:, 7] = 0
    return pack(x, b, o, w, t)
def setup_inputs_corners(rng):
    a = (np.arange(65536)[:, None] >> np.arange(16)) & 1
    par = np.stack([(np.arange(16) >> i) & 1 for i in range(4)] + [np.ones(16, np.int64)], axis=1)
    words = a[~np.any(((a @ par) & 1) == 1, axis=1)]
    few = words[np.sum(words, axis=1) <= 10]
    src = (N - 2 - (A - 1) % (N - 1)) % N
    late = (5 - A) * L
    x = rng.integers(100, 132, (N, 8, 16, W)); b = rng.integers(0, W, (N, 8, 16, W)); o = np.zeros((N, 8, Q), np.int64)
    far = np.arange(W) + 1 + rng.integers(W // 4, 3 * W // 4, (N, 8, W)); far = far & (W - 1); far = far - (far & 1); b[:, :, 0] = (far - 1) & (W - 1)
    for q in range(N):
        for g in range(8):
            n = int(rng.choice(np.array([0, 1, U - 1, U, U + 1, L])))
            if q == 0: n = (U, U + 1, L, U - 1, 1, 0, U, L)[g]
            if g == 4: n = U if q == src else 1 if q == (src + 1) % N else int(rng.choice(np.array([0, 1, U - 1, U])))
            if g == 5: n = 0
            odd = rng.permutation(W // 2) * 2 + 1; even = np.arange(W // 2) * 2
            rest = rng.permutation(np.concatenate([odd[n:], even]))
            first = rng.permutation(np.concatenate([odd[:n], rest[:L - n]])); more = rest[L - n:]
            o[q, g] = (np.concatenate([more[:late], first, more[late:]]) if g == 7 else np.concatenate([first, more]))[:Q]
            lone = np.zeros(W, bool)
            if g != 4 and g != 7: lone[odd[n:][rng.random(W // 2 - n) < 0.1]] = True
            lone[rest[:L - n]] = False; lone[odd[:n]] = True
            k = int(np.count_nonzero(lone))
            if g == 4: x[q, g][:, lone] = 30 + 160 * few[rng.permutation(few.shape[0])[:k]].T
            else: x[q, g][:, lone] = 255 * words[rng.permutation(2048)[:k]].T
            if g == 4 and q == src: x[q, g][:, first[np.flatnonzero(lone[first])[-1]]] = 255
    w = np.zeros((N, 8, 16), np.int64) + rng.choice(np.array([0, 1, 255]), (N, 8, 1)); w[:, 3] = 255; w[:, 2] = 0
    t = rng.choice(np.array([600, 600, 600, 0]), (N, 8)); t[0] = 600; t[1, 6] = 0; t[:, 4] = 600; t[:, 5] = 4095; t[:, 7] = 600
    return pack(x, b, o, w, t)
def setup_inputs_ties(rng):
    _, b, o, w, t = parts(rng)
    kd = np.repeat(rng.random((N, 8, W // 2)), 2, axis=-1); half = np.argsort(rng.random((N, 8, 16, W)), axis=2) < 8; kx = kd[:, :, None, :]
    x = np.where(kx < 0.35, 100, np.where(kx < 0.7, 140, np.where(half, 100, 140)))
    for q in range(N):
        for g in range(8):
            com = np.flatnonzero(kd[q, g, ::2] < 0.7) * 2
            b[q, g] = np.where(rng.random((16, W)) < 0.05, b[q, g], com[rng.integers(0, com.shape[0], (16, W))])
    t = rng.choice(np.array([0, 319, 320, 321]), (N, 8)); t[0, :4] = np.array([0, 319, 320, 321]); t[1, 4:] = np.array([320, 321, 0, 320])
    return pack(x, b, o, w, t)
def setup_inputs_near(rng):
    _, b, o, w, t = parts(rng)
    y = (np.add.accumulate(rng.integers(-3, 4, (N, 8, 16, W)), axis=3) + rng.integers(0, 512, (N, 8, 16, 1))) & 511
    x = np.where(y > 255, 511 - y, y); u = np.arange(W)
    b = np.where(rng.random((N, 8, 16, W)) < 0.7, (u + rng.choice(np.array([-17, -16, -15, -1, 0, 1, 15, 16, 17]), (N, 8, 16, W))) & (W - 1), b)
    b = np.where(rng.random((N, 8, 1, W)) < 0.25, (u + rng.integers(-15, 16, (N, 8, 16, W))) & (W - 1), b)
    key = rng.random((N, 8, W)); key[..., :16] -= 1; key[..., W - 16:] -= 1; o = np.argsort(key, axis=-1)[..., :Q]
    t = rng.choice(np.array([40, 100, 400, 900, 4095]), (N, 8)); t[0, 0] = 4095; t[0, 1] = 40; t[1, 2] = 100
    return pack(x, b, o, w, t)
def check_inputs(d):
    bad = []
    for k, lo, hi in (("xs", 0, 255), ("nb", 0, W - 1), ("od", 0, W - 1), ("wt", 0, 255), ("th", 0, 4095)):
        a = np.asarray(d[k]).astype(np.float32)
        if not (np.min(a) >= lo and np.max(a) <= hi): bad.append("range of " + k)
    a = np.asarray(d["xs"]).astype(np.float32)
    if np.any(a != np.floor(a)): bad.append("whole numbers in xs")
    o = np.sort(np.stack([gentries(a) for a in d["od"]]), axis=-1)
    if np.any(o[..., 1:] == o[..., :-1]): bad.append("different numbers in a group's od")
    return bad
def dist(X, c, x):
    n = c.shape[3]
    e = np.take_along_axis(X, c.reshape(N, 8, 1, 16 * n), 3).reshape(N, 8, 16, 16, n)
    return np.add.reduce(np.abs(e - x[:, :, :, None, :]), axis=2)
def reference(xs, nb, od, wt, th):
    X = xs.astype(np.float32).astype(np.int64).reshape(N, 8, 16, W); col = nb.astype(np.int64).reshape(N, 8, 16, W)
    order = np.stack([gentries(a) for a in od]).astype(np.int64); w = wt.astype(np.int64).reshape(N, 8, 16, 1); lim = th.astype(np.int64).reshape(N, 8)
    v = np.zeros((N, 8, L), np.int64); m = np.zeros((N, 8, L), np.int64); age = np.zeros((N, 8, L), np.int64); c = np.zeros((N, 8, 16, L), np.int64)
    free = np.ones((N, 8, L), bool); cur = np.zeros((N, 8, 1), np.int64); gx = np.zeros((N, 8, 16, U), np.int64); gm = np.zeros((N, 8, U), np.int64)
    seen = []; judged = gm
    for t in range(T):
        f = free.astype(np.int64); run = np.add.accumulate(f, axis=2)
        v = np.where(free, np.take_along_axis(order, np.minimum(cur + run - f, Q - 1), 2), v); cur = cur + run[:, :, L - 1:]
        m = np.where(free, 4095, m); age = np.where(free, 0, age)
        seed = (np.take_along_axis(col, ((v - 1) & (W - 1))[:, :, None, :], 3) + 1) & (W - 1)
        c = np.where(free[:, :, None, :], seed, c)
        h = (np.add.reduce(w * gx, axis=2) + 77 * t) & (W - 1)
        gc = np.take_along_axis(col, h[:, :, None, :], 3)
        own = np.take_along_axis(X, v[:, :, None, :], 3)
        D = np.where(np.abs(c - v[:, :, None, :]) < 16, 4095, dist(X, c, own))
        m = np.minimum(m, np.min(D, axis=2)); near = np.take_along_axis(c, np.argmin(D, axis=2)[:, :, None, :], 2)
        judged = np.minimum(gm, np.min(dist(X, gc, gx), axis=2))
        np.put_along_axis(col, v[:, :, None, :], c, 3)
        alive = m >= lim[:, :, None]; age = np.where(alive, age + 1, age)
        go = (alive & (age >= A)).astype(np.int64); before = np.add.accumulate(go, axis=2) - go
        leave = (go == 1) & (before < U) & (t < T - 1)
        c = np.take_along_axis(col, near, 3)
        free = ~alive | leave
        slot = np.where(leave, before, U); nx = np.zeros((N, 8, 16, U + 1), np.int64); nm = np.zeros((N, 8, U + 1), np.int64)
        np.put_along_axis(nx, slot[:, :, None, :], own, 3); np.put_along_axis(nm, slot, m, 2)
        gx = np.roll(nx[..., :U], 1 + t % (N - 1), axis=0); gm = np.roll(nm[..., :U], 1 + t % (N - 1), axis=0)
        best = np.max(judged, axis=(0, 2)); lim = lim + (np.maximum(best[None, :] - lim, 0) >> 2)
        seen.append(lim)
    yn = np.take_along_axis(col, order[:, :, None, :K], 3).reshape(N, 128, K)
    return {"yn": yn.astype(np.float32), "yv": v.astype(np.float32), "ym": m.astype(np.float32), "yg": judged.astype(np.float32), "yt": np.stack(seen, axis=2).astype(np.float32)}

@@ -1,0 +1,803 @@
+import numpy as np
+from concourse.bass import DstId, RemoteDMATransfer
+from concourse.mybir import dt, AluOpType, AxisListType, ActivationFunctionType
+
+W, L, U, NT, Q = 2048, 160, 96, 6, 960
+f32, bf, i32, u16, f16 = "float32", "bfloat16", "int32", "uint16", "float16"
+SB = {
+    "X": (W, bf), "colx": (L + W, i32), "odl": (60, i32), "wtl": (1, i32), "thl": (1, i32),
+    "od16": (60, u16), "odf": (60, f32), "jj16": (60, u16), "odD": (320, f32), "ptmp": (320, f32),
+    "P1": (Q, bf), "Xo": (Q, bf), "own0": (L, bf), "own1": (L, bf), "vp": (L, bf), "nxp": (L, bf),
+    "a": (16 * L, bf), "mx": (16 * L, bf), "ga0": (16 * L, bf), "ga1": (16 * L, bf), "gab": (16 * L, bf),
+    "v160": (10, u16), "v161": (10, u16), "c16": (L, u16), "cF0": (L, f32), "cF1": (L, f32), "dd": (L, f32), "ad": (L, bf), "pen": (L, bf), "yy": (L, bf),
+    "TK": (L, f32), "TD": (L, f32), "S": (2 * L, f32), "patA": (L, f32),
+    "fI": (50, bf), "go": (10, bf), "d5": (50, f32), "s5": (50, f16), "I20": (20, i32), "lo20": (20, i32),
+    "mulc": (20, f32), "off1": (10, u16), "off2": (10, u16), "pt": (10, f32), "pos0": (10, f32), "pos1": (10, f32),
+    "cur0": (1, f32), "cur1": (1, f32), "fl": (10, bf), "nfr": (1, f32), "nx16": (10, u16),
+    "vi": (10, i32), "vj": (10, i32), "sd16": (10, u16), "v16": (10, u16), "stmp": (L, i32), "stm2": (L, i32),
+    "st1": (10, f32), "st2": (10, f32), "slT": (10, f16), "sl16": (10, u16),
+    "mS": (10, f32), "mG": (10, f32), "mOld": (10, f32), "oPM": (10, f32), "nF": (10, f32),
+    "thT": (10, f32), "thr": (10, f32), "tS": (10, f32), "tG": (10, f32), "tA": (10, f32), "tu": (10, f32), "tv": (10, f32),
+    "mL": (10, f32), "mD": (L, f32), "mw": (256, f32), "lv0": (20, f32), "lv1": (20, f32), "st3": (10, f32), "gJ": (10, f32),
+    "hi": (10, i32), "hj": (10, i32), "h16": (10, u16), "gc160": (L, u16), "gc161": (L, u16), "gT": (L, f32), "GS0": (L, f32), "GS1": (L, f32), "BON0": (128, bf), "BON6": (128, bf),
+    "JT": (32, f32), "JU": (32, f32), "br": (1, f32), "b1": (1, f32), "b2": (1, i32), "b3": (1, i32),
+    "thK": (8, f32), "tho": (8, f32), "thf": (1, f32), "wf": (1, f32),
+    "oi": (10, i32), "oj": (10, i32), "ok": (10, i32), "ol": (10, i32), "om": (32, f32), "omT": (32, f32), "og": (10, f32), "ogT": (U, f32),
+    "ov": (L, f32), "on": (Q, f32),
+    "pI": (1, i32), "pJ": (4, i32), "pK": (1, i32), "pf": (1, f32), "pc": (12, f32), "pd": (2, f32),
+    "Dg": (128, f32), "g16": (128, f32), "g32": (128, f32),
+    "xs1": (144, f32), "xm16": (320, f32), "ln": (10, f32), "qq": (10, f32), "gg": (10, f32), "jjI": (60, i32),
+    "SEL1": (144, bf), "SEL2": (144, bf), "SELN": (144, bf), "SELW": (144, bf),
+    "BO": (128, bf), "BON16": (128, bf), "BON4": (128, bf), "BON8": (128, bf), "BON10": (128, bf), "BON12": (128, bf), "BON14": (128, bf), "BOf": (128, f32), "Ib": (128, bf), "In": (128, bf), "Iy": (128, bf), "If": (128, f32),
+    "KC": (128, bf), "DC": (128, bf), "DM": (128, f32), "DY": (128, bf), "ones": (L, bf), "cy": (128, bf), "cn": (128, bf), "onef": (128, f32),
+    "L32": (128, bf), "O32": (128, bf), "O32f": (128, f32), "LG": (128, bf), "OG": (128, bf), "tm": (128, f32), "tn": (128, f32),
+    "PL": (128, f32), "mask": (320, f32), "mBIG": (L, f32), "lane96": (10, f32), "qrev": (10, f32), "ggm": (10, f32), "CT": (50, f32),
+}
+for _h in range(2):
+    for _g in range(2):
+        SB["PH%d%d" % (_h, _g)] = (128, f16)
+        SB["PF%d%d" % (_h, _g)] = (128, f32)
+for _t in range(2, NT):
+    SB["gx%d" % _t] = (L, bf)
+    SB["gm%d" % _t] = (20, f32)
+    SB["rb%d" % _t] = (12, f32)
+PLACE, FILL = {}, {}
+for _k, (_n, _d) in SB.items():
+    if _n > 320:
+        PLACE[_k] = (_k, 0)
+    else:
+        PLACE[_k] = ("m_" + _d, FILL.get(_d, 0))
+        FILL[_d] = FILL.get(_d, 0) + -(-_n // 16) * 16
+SCRATCH = {k: ("sbuf", [128, n], d) for k, (n, d) in SB.items() if n > 320}
+for _d, _n in FILL.items():
+    SCRATCH["m_" + _d] = ("sbuf", [128, _n], _d)
+for _b in range(8):
+    SCRATCH["ps%d" % _b] = ("psum", [128, 512], f32)
+NDMA = 30
+SEMAPHORES = ["sV", "sS", "sP", "sG"] + ["d%d" % k for k in range(NDMA)] \
+    + ["%s%d" % (n, t) for n in ("ax", "am", "ab", "lx", "lm", "lb") for t in range(2, NT)]
+BYTES = {f32: 4, bf: 2, i32: 4, u16: 2, f16: 2}
+OPT = {"cuts": [[(0, 40, "S"), (40, 80, "V"), (80, 130, "S"), (130, 160, "V")], [(0, 40, "S"), (40, 80, "V"), (80, 120, "S"), (120, 160, "S")]]
+       + [[(0, 40, "S"), (40, 64, "V"), (64, 80, "S"), (80, 120, "S"), (120, 160, "S")]] * 3
+       + [[(0, 40, "S"), (40, 80, "S"), (80, 120, "S"), (120, 160, "S")]],
+       "chunks": [[0, 80, 160]] * 6, "gcuts": [[(0, 40, "S"), (40, 80, "S"), (80, 120, "S"), (120, 160, "S")]] * 6,
+       "kv": [0, 0, 10, 10, 10, 10], "ko": [14, 14, 12, 12, 12, 16],
+       "seed": 1, "noise": 0.5, "rounds": 30, "moves": 1300, "slack": 300.0, "onS": "abdegij", "dd": "P",
+       "wake": 120.0, "far": 3500.0, "fan": 6500.0, "gather": 1.56, "scatter": 3.8}
+PLAN = {}
+
+
+def arrange(nodes):
+    n = len(nodes)
+    x = [OPT["seed"] * 7919 + 1]
+
+    def rnd():
+        x[0] = (x[0] * 1103515245 + 12345) % 2147483648
+        return x[0] / 2147483648.0
+    qs = [nd["q"] for nd in nodes]
+    pred = [[(d, 0.0 if qs[d] == nd["q"] == "P" else OPT["wake"]) for d in nd["deps"]] for nd in nodes]
+    succ = [[] for nd in nodes]
+    for i in range(n):
+        for d, w in pred[i]:
+            succ[d].append((i, w))
+
+    wake = OPT["wake"]
+    banks = [([r[0] for it in nd["items"] for r in it["reads"] + it["writes"] if r[0] not in SB] + [None])[0] for nd in nodes]
+
+    def first(slots, t):
+        lo, hi = 0, len(slots)
+        while lo < hi:
+            mid = (lo + hi) // 2
+            if slots[mid][1] <= t:
+                lo = mid + 1
+            else:
+                hi = mid
+        return lo
+
+    def place(prio, back, noise):
+        start, end, busy = [0.0] * n, [0.0] * n, {}
+        for i in sorted(range(n), key=lambda j: (-prio[j], -j if back else j)):
+            dur, lat = nodes[i]["dur"], nodes[i]["lat"]
+            if noise:
+                dur *= 1 + noise * (2 * rnd() - 1)
+            t = max([end[d] + w for d, w in (succ if back else pred)[i]] + [0.0]) + (lat if back else 0.0)
+            if qs[i]:
+                slots, b = busy.setdefault(qs[i], []), banks[i]
+                while True:
+                    lo = first(slots, t)
+                    while lo < len(slots) and slots[lo][0] < t + dur:
+                        t = max(t, slots[lo][1])
+                        lo += 1
+                    if b is None:
+                        break
+                    uses, was = busy.setdefault(b, []), t
+                    k = first(uses, t - wake)
+                    while k < len(uses) and uses[k][0] < t + dur + wake:
+                        if uses[k][2] != qs[i]:
+                            t = max(t, uses[k][1] + wake)
+                        k += 1
+                    if t == was:
+                        uses.insert(first(uses, t), (t, t + dur, qs[i]))
+                        break
+                slots.insert(lo, (t, t + dur))
+            start[i], end[i] = t, t + dur + (0.0 if back else lat)
+        return start, end
+
+    level = [0.0] * n
+    for i in range(n - 1, -1, -1):
+        level[i] = nodes[i]["dur"] + nodes[i]["lat"] + max([level[j] + w for j, w in succ[i]] + [0.0])
+    best = place(level, False, 0.0)
+    for it in range(OPT["rounds"]):
+        now = place(place(best[1], True, OPT["noise"])[1], False, 0.0)
+        if max(now[1]) <= max(best[1]) + OPT["slack"] * (1 - it / OPT["rounds"]):
+            best = now
+    marks = [i for i in range(n) if qs[i] is None]
+    kinds = {}
+    for i in range(n):
+        if qs[i] and nodes[i]["items"][0]["writes"]:
+            kinds.setdefault((qs[i], nodes[i]["items"][0]["writes"][0][0], nodes[i]["step"]), []).append(i)
+    kinds = list(kinds.values())
+    kind = {i: k for k in range(len(kinds)) for i in kinds[k]}
+    seen = [None, None]
+
+    def score(p):
+        return max(p[1]) + 0.3 * sum(p[1][i] for i in marks) / len(marks)
+
+    top = best
+    for it in range(OPT["moves"]):
+        key = list(best[0])
+        if seen[0] is not best:
+            ends = {(qs[i], round(best[0][i] + nodes[i]["dur"])): i for i in range(n) if qs[i]}
+            pairs, i = [], max(range(n), key=lambda j: best[1][j])
+            while i is not None:
+                d = max(pred[i], key=lambda e: best[1][e[0]] + e[1]) if pred[i] else None
+                if d is not None and best[1][d[0]] + d[1] + 1 >= best[0][i]:
+                    i = d[0]
+                else:
+                    j = ends.get((qs[i], round(best[0][i])))
+                    if j is not None and kind.get(j) != kind.get(i):
+                        pairs.append((j, i))
+                    i = j
+            seen[0], seen[1] = best, pairs
+        if seen[1] and rnd() < 0.75:
+            j, i = seen[1][int(rnd() * len(seen[1]))]
+            by = 3000.0 * rnd() * rnd() + 100
+            way = rnd()
+            if way < 0.6 and j in kind:
+                s = 1 if way < 0.3 else -2
+                for e in kinds[kind[j]]:
+                    key[e] += s * by
+            elif i in kind:
+                for e in kinds[kind[i]]:
+                    key[e] -= by
+        else:
+            by = (rnd() - 0.65) * 6000.0 * rnd()
+            for i in kinds[int(rnd() * len(kinds))]:
+                key[i] += by
+        for i in range(n - 1, -1, -1):
+            for j, w in succ[i]:
+                if key[i] >= key[j]:
+                    key[i] = key[j] - 1.0
+        now = place([-k for k in key], False, 0.0)
+        if it % 8 == 7:
+            now = place(place(now[1], True, 0.2)[1], False, 0.0)
+        if score(now) <= score(best) + OPT["slack"] * (1 - it / OPT["moves"]) * rnd():
+            best = now
+            if score(now) < score(top):
+                top = now
+    start, end = top
+    PLAN["times"] = (start, end)
+    PLAN["nodes"] = nodes
+    return sorted(range(n), key=lambda j: (start[j], j))
+
+
+def rank_program(g, core, T, topo):
+    rank = T.rank_of(core)
+    if rank is None:
+        return
+    N = len(T.cores)
+    Op, Fn = AluOpType, ActivationFunctionType
+    QU = {"V": g.vector, "S": g.scalar, "P": g.tensor, "G": g, "Y": g.sync}
+    size = {k: n for k, (n, d) in SB.items()}
+    size.update({"ps%d" % b: 512 for b in range(8)})
+    nodes, macro, group, ndma, step = [], [], {}, [0], [-1]
+    nwr = {k: np.full(n, -1) for k, n in size.items()}
+    nrd = {k: [] for k in size}
+
+    def A(name, a=0, b=None, s=1, p=None):
+        if b is None:
+            b = size[name]
+        ps = slice(0, 128) if p is None else p
+        buf, o = PLACE.get(name, (name, 0))
+        two = name in SB and BYTES[SB[name][1]] == 2
+        return {"ap": T[buf][ps, o + a:o + b:s] if s != 1 else T[buf][ps, o + a:o + b], "r": [(name, slice(a, b, s))],
+                "n": len(range(a, b, s)), "two": two, "ps": name not in SB}
+
+    def IND(win, off):
+        return {"ap": win["ap"].indirect(off["ap"]), "r": win["r"], "x": off["r"], "n": 16 * off["n"], "two": False, "ps": False}
+
+    def wide(reg):
+        name, sl = reg
+        e = 16 // BYTES[SB[name][1]]
+        return name, slice(sl.start // e * e, min(-(-sl.stop // e) * e, size[name]), 1)
+
+    def node(q, items, dur, lat=0.0, acc=None, after=()):
+        reads = [r for it in items for r in it["reads"]]
+        writes = [r for it in items for r in it["writes"]]
+        me, deps = len(nodes), set(after)
+        if acc in ("mid", "stop"):
+            name = writes[0][0]
+            deps.update(group[name]["ops"] if acc == "stop" else group[name]["ops"][:1])
+            group[name]["ops"].append(me)
+            writes = group[name]["regs"] if acc == "stop" else []
+        for name, sl in reads + writes:
+            deps.update(int(o) for o in np.unique(nwr[name][sl]))
+        for name, sl in writes:
+            mark = np.zeros(size[name], bool)
+            mark[sl] = True
+            deps.update(o for o, s2 in nrd[name] if mark[s2].any())
+        if acc == "start":
+            group[writes[0][0]] = {"ops": [me], "regs": list(writes)}
+        for name, sl in reads:
+            nrd[name].append((me, sl))
+        for name, sl in writes:
+            nwr[name][sl] = me
+            mark = np.zeros(size[name], bool)
+            mark[sl] = True
+            nrd[name] = [(o, s2) for o, s2 in nrd[name] if o == me or not mark[s2].all()]
+        deps.discard(-1)
+        deps.discard(me)
+        nodes.append({"q": q, "items": items, "dur": dur, "lat": lat, "deps": sorted(deps), "step": step[0]})
+        return me
+
+    def call(q, fn, out, ins, per=None, acc=None):
+        reads, writes = list(out.get("x", [])), list(out["r"])
+        ins = [x for x in ins if isinstance(x, dict)]
+        for x in ins:
+            reads += x["r"] + x.get("x", [])
+        n = max(out["n"], ins[0]["n"] if ins else 0)
+        if q == "P":
+            dur = max(64, out["n"]) * (0.5 if ins[0]["two"] else 2.0)
+        elif q == "G":
+            dur = 150.0 + 2 * n
+        elif "x" in out:
+            dur = 50.0 + out["n"] * OPT["scatter"]
+        elif ins and "x" in ins[0]:
+            dur = 60.0 + out["n"] * OPT["gather"]
+        elif q == "S":
+            dur = 65.0 + n
+        else:
+            dur = max(64.0, n * (per or (0.5 if all(x["two"] or x["n"] == 1 for x in [out] + ins) else 1.0)))
+        it = {"kind": "c", "q": q, "fn": fn, "reads": reads, "writes": writes}
+        if macro:
+            macro[0].append(it)
+            macro[1] += dur
+        else:
+            node(q, [it], dur, acc=acc)
+
+    def together(q, body):
+        macro.extend([[], 0.0])
+        body()
+        items, dur = macro
+        del macro[:]
+        node(q, items, dur)
+
+    def emit(seq):
+        cnt = {"V": 0, "S": 0, "P": 0, "G": 0}
+        known = {q: {} for q in QU}
+        done, tails = [], {}
+        wr = {k: np.full(n, -1) for k, (n, d) in SB.items()}
+        rd = {k: {} for k in SB}
+        bank = {"ps%d" % b: {} for b in range(8)}
+
+        def order(q, eng, reads, writes):
+            deps = set()
+            for name, sl in reads + writes:
+                if name in bank:
+                    deps.update(o for e, o in bank[name].items() if e != eng)
+                else:
+                    deps.update(int(o) for o in np.unique(wr[name][sl]))
+            for name, sl in writes:
+                if name not in bank:
+                    for arr in rd[name].values():
+                        deps.update(int(o) for o in np.unique(arr[sl]))
+            deps.discard(-1)
+            for o in sorted(deps, reverse=True):
+                sem, c, clock = done[o]
+                if known[q].get(sem, 0) < c:
+                    QU[q].wait_ge(T.sem[sem], c)
+                    for k2, c2 in clock.items():
+                        if known[q].get(k2, 0) < c2:
+                            known[q][k2] = c2
+
+        def note(q, eng, sem, c, reads, writes):
+            clock = dict(known[q]) if q else {}
+            clock[sem] = c
+            done.append((sem, c, clock))
+            o = len(done) - 1
+            tails[sem] = c
+            for name, sl in reads + writes:
+                if name in bank:
+                    bank[name][eng] = o
+            for name, sl in reads:
+                if name not in bank:
+                    if eng not in rd[name]:
+                        rd[name][eng] = np.full(size[name], -1)
+                    rd[name][eng][sl] = o
+            for name, sl in writes:
+                if name not in bank:
+                    wr[name][sl] = o
+                    for arr in rd[name].values():
+                        arr[sl] = -1
+
+        for i in seq:
+            for it in nodes[i]["items"]:
+                q = it["q"]
+                if it["kind"] == "c":
+                    order(q, q, it["reads"], it["writes"])
+                    cnt[q] += 1
+                    it["fn"]().then_inc(T.sem["s" + q], 1)
+                    note(q, q, "s" + q, cnt[q], it["reads"], it["writes"])
+                elif it["kind"] == "in":
+                    note(None, it["sem"], it["sem"], it["c"], [], it["writes"])
+                else:
+                    order(q, it["sem"], it["reads"], it["writes"])
+                    it["fn"]()
+                    note(q, it["sem"], it["sem"], it["c"], it["reads"], it["writes"])
+        for sem, c in tails.items():
+            if known["G"].get(sem, 0) < c:
+                g.wait_ge(T.sem[sem], c)
+
+    def ap(x):
+        return x["ap"] if isinstance(x, dict) else x
+
+    def cp(out, in_):
+        call("V", lambda: g.vector.tensor_copy(out["ap"], in_["ap"]), out, [in_])
+
+    def tt(out, a, b, op):
+        call("V", lambda: g.vector.tensor_tensor(out["ap"], a["ap"], b["ap"], op), out, [a, b], per=1.0 if a["ps"] or b["ps"] else 2.0)
+
+    def ts(out, a, s1, o1, s2=None, o2=None):
+        if o2 is None:
+            call("V", lambda: g.vector.tensor_scalar(out["ap"], a["ap"], ap(s1), None, o1), out, [a, s1])
+        else:
+            call("V", lambda: g.vector.tensor_scalar(out["ap"], a["ap"], ap(s1), ap(s2), o1, o2), out, [a, s1, s2])
+
+    def scan(out, d0, d1, init, o0, o1):
+        call("V", lambda: g.vector.tensor_tensor_scan(out["ap"], d0["ap"], d1["ap"], init, o0, o1), out, [d0, d1])
+
+    def red(out, in_, op):
+        call("V", lambda: g.vector.tensor_reduce(out["ap"], in_["ap"], AxisListType.X, op), out, [in_])
+
+    def tr(out, in_):
+        call("V", lambda: g.vector.transpose(out["ap"], in_["ap"]), out, [in_])
+
+    def act(out, in_, fn, bias=0.0, scale=1.0):
+        call("S", lambda: g.scalar.activation(out["ap"], in_["ap"], fn, bias=ap(bias), scale=ap(scale)), out, [in_, bias, scale])
+
+    def aff(tag, out, in_, scale, bias):
+        if tag in OPT["onS"]:
+            act(out, in_, Fn.Identity, bias, scale)
+        else:
+            ts(out, in_, scale, Op.mult, bias, Op.add)
+
+    def gather(on, out, win, off):
+        x = IND(win, off)
+        if on == "S":
+            call("S", lambda: g.scalar.activation(out["ap"], x["ap"], Fn.Copy), out, [x])
+        else:
+            cp(out, x)
+
+    def mm(out, lhsT, rhs, start, stop):
+        call("P", lambda: g.tensor.matmul(out["ap"], lhsT["ap"], rhs["ap"], start, stop), out, [lhsT, rhs],
+             acc=None if start and stop else "start" if start else "stop" if stop else "mid")
+
+    def iota(out, pat, base, cm):
+        if SB[out["r"][0][0]][1] == i32:
+            call("G", lambda: g.iota(out["ap"], pat, base, cm), out, [])
+        else:
+            call("G", lambda: g.iota(out["ap"], pat, base, cm, allow_small_or_imprecise_dtypes=True), out, [])
+
+    def fill(out, c):
+        iota(out, [[0, out["n"]]], c, 0)
+
+    def diag(out, in_):
+        call("G", lambda: g.affine_select(out["ap"], in_["ap"], [[-1, 128]], Op.is_equal, 0.0, 0, 1), out, [in_])
+
+    def dma(q, out, in_, lat=2500.0):
+        sem = "d%d" % ndma[0]
+        ndma[0] += 1
+        reads = [wide(r) for r in in_["r"]] if isinstance(in_, dict) else []
+        writes = [wide(r) for r in out["r"]] if isinstance(out, dict) else []
+        node(q, [{"kind": "d", "q": q, "sem": sem, "c": 16, "reads": reads, "writes": writes,
+                  "fn": lambda: QU[q].dma_start(ap(out), ap(in_)).then_inc(T.sem[sem], 16)}], 100.0, lat)
+
+    def remote(fn, src, lsem, nl, dst, rsem, nr, lat):
+        me = node("G", [{"kind": "r", "q": "G", "sem": lsem, "c": nl, "reads": [wide(r) for r in src["r"]], "writes": [], "fn": fn}], 1000.0, lat)
+        node(None, [{"kind": "in", "q": None, "sem": rsem, "c": nr, "reads": [], "writes": dst["r"]}], 1.0, 0.0, after=[me])
+
+    def bits(m):
+        return bin(m).count("1")
+
+    def send(src, dstbuf, shift, rsem, lsem):
+        to, fr = T.cores[(rank + shift) % N], T.cores[(rank - shift) % N]
+        rid, pid, _ = topo.addr(to)
+        m = topo.mask(core, to)
+        remote(lambda: g.remote_dma(dstbuf["ap"], src["ap"], T.sem[rsem], T.sem[lsem], pid, rid, m),
+               src, lsem, bits(m), dstbuf, rsem, bits(topo.mask(fr, core)), OPT["far"])
+
+    def fan_plan(c):
+        far = [x for x in T.cores if topo.chip(x) != topo.chip(c)]
+        near = [x for x in T.cores if topo.chip(x) == topo.chip(c) and x != c]
+        mf = -1
+        for x in far:
+            mf &= topo.mask(c, x)
+        plan = [(far, mf)]
+        if near:
+            es = [e for e in topo.engines(c, near[0]) if not mf >> e & 1][:2]
+            plan.append((near, sum(1 << e for e in es)))
+        return plan
+
+    def send_all(src, name, rsem, lsem):
+        trs, tot = [], 0
+        for dsts, m in fan_plan(core):
+            js = [(T.rank_of(x) - rank - 1) % N for x in dsts]
+            trs.append(RemoteDMATransfer(dst_ids=[DstId(rid=topo.addr(x)[0], pnc=topo.addr(x)[1]) for x in dsts],
+                                         dma_engine_mask=m, remote_sem=T.sem[rsem], src=src["ap"],
+                                         dsts=[A(name, 4 + j, 5 + j)["ap"] for j in js]))
+            tot += bits(m)
+        got = sum(bits(m) for x in T.cores if x != core for dsts, m in fan_plan(x) if core in dsts)
+        remote(lambda: g.remote_dma_fused(trs, local_sem=T.sem[lsem]), src, lsem, tot, A(name, 4, 3 + N), rsem, got, OPT["fan"])
+
+    def PS(b, a, e, s=1):
+        return A("ps%d" % b, a, e, s)
+
+    def sel(name, r):
+        return A(name, 15 - r, 143 - r)
+
+    def pc(j):
+        return A("pc", j, j + 1)
+
+    def to_list(out, name, src, n):
+        together("P", lambda: [mm(out, sel(name, r), A(src, r, n, 16), r == 0, r == 15) for r in range(16)])
+
+    def swap(b, a, kind, src, e, stride):
+        together("P", lambda: [mm(PS(b, a + h, a + 10, 2), A("%s%d%d" % (kind, h, gg)), A(src, stride * gg + e, 10 * stride, 2 * stride),
+                                  gg == 0, gg == 1) for h in range(2) for gg in range(2)])
+
+    col = A("colx", L, L + W)
+    BIG = 8192.0
+
+    dma("S", A("odl"), T.od[:])
+    dma("Y", col, T.nb[:], 7000.0)
+    dma("Y", A("X"), T.xs[:], 9500.0)
+    nodes[-2]["items"] += nodes[-1]["items"]
+    nodes[-1].update({"q": None, "items": [], "dur": 2500.0, "lat": 0.0, "deps": [len(nodes) - 2]})
+    dma("S", A("thl", p=slice(0, 8)), T.th[:])
+    dma("S", A("wtl"), T.wt[:])
+
+    iota(A("pI"), [[0, 1]], 0, 1)
+    iota(A("pf"), [[0, 1]], 0, 1)
+    iota(A("jjI"), [[1, 60]], 0, 0)
+    iota(A("xm16"), [[0, 20], [1, 16]], 0, 0)
+    iota(A("g16"), [[16, 8], [0, 16]], 0, 0)
+    iota(A("Dg"), [[1, 128]], 0, -1)
+    iota(A("xs1"), [[1, 144]], -15, 0)
+    iota(A("g32"), [[32, 4], [0, 32]], 0, 0)
+    iota(A("ln"), [[32, 5], [0, 2]], U, 1)
+    iota(A("qq"), [[16, 10]], 0, 1)
+    iota(A("gg"), [[0, 5], [1, 2]], 0, 0)
+    iota(A("PL"), [[1, 128]], 0, 0)
+    fill(A("ones"), 1)
+    fill(A("onef"), 1)
+    fill(A("cn"), -1)
+    diag(A("Ib"), A("ones", 0, 128))
+    diag(A("If"), A("onef"))
+    diag(A("In"), A("cn"))
+    fill(A("patA"), 0)
+    fill(A("patA", 15, L, 16), int(BIG))
+    fill(A("CT"), -2048)
+    fill(A("CT", 0, 50, 5), int(160.5 * BIG))
+    fill(A("fI"), 0)
+    fill(A("d5"), 2048)
+    fill(A("d5", 4, 50, 5), -2048)
+    fill(A("mulc", 0, 10), 65536)
+    fill(A("mulc", 10, 20), 1024)
+    fill(A("cur0"), L - 1)
+    fill(A("nF"), 4095 + int(BIG))
+    fill(A("mG"), -65536)
+    fill(A("mOld"), 4095 + int(BIG))
+    for name in ("mw", "JT", "om") + (("BON0",) if 0 in OPT["kv"][2:] else ()):
+        fill(A(name), 0)
+    for j, m in enumerate((112, 96, 15, 16)):
+        ts(A("pJ", j, j + 1), A("pI"), m, Op.bitwise_and)
+    cp(A("pc", 0, 4), A("pJ"))
+    cp(A("jj16"), A("jjI"))
+    ts(A("mask"), A("xm16"), pc(2), Op.is_equal)
+    ts(pc(4), pc(2), -128.0, Op.mult)
+    ts(A("BOf"), A("g16"), pc(0), Op.is_equal)
+    cp(A("odf"), A("odl"))
+    cp(A("od16"), A("odl"))
+
+    def table(j):
+        tt(A("odD"), IND(A("odf"), A("jj16", 20 * j, 20 * j + 20)), A("mask"), Op.mult)
+        mm(PS(6 + j % 2, 0, 320), A("BOf"), A("odD"), True, True)
+        act(A("ptmp"), PS(6 + j % 2, 0, 320), Fn.Relu, bias=pc(4))
+        act(A("P1", 320 * j, 320 * j + 320), A("ptmp"), Fn.Relu, bias=128.0, scale=-1.0)
+
+    for j in range(3):
+        table(j)
+    ts(A("vi"), A("odl", 0, 10), 2047.0, Op.add)
+    ts(A("vj"), A("vi"), 2047, Op.bitwise_and)
+    cp(A("sd16"), A("vj"))
+    ts(A("BO"), A("g16"), pc(0), Op.is_equal)
+    ts(A("BON16"), A("g16"), pc(0), Op.is_equal, -1.0, Op.mult)
+    for kv in sorted(set(OPT["kv"][2:] + OPT["ko"]) - {0, 16}):
+        ts(A("tn"), A("xm16", 0, 128), float(kv), Op.is_lt)
+        tt(A("BON%d" % kv), A("tn"), A("BON16"), Op.mult)
+    ts(A("SEL2"), A("xs1"), pc(0), Op.is_equal, 2.0, Op.mult)
+    ts(A("SELN"), A("xs1"), pc(0), Op.is_equal, -1.0, Op.mult)
+    ts(A("SEL1"), A("xs1"), pc(0), Op.is_equal)
+    ts(A("Iy"), A("Ib"), 1.0 / 1024, Op.mult)
+    ts(pc(5), pc(2), -3.0, Op.add, 1.0 / 16, Op.mult)
+    ts(pc(6), pc(2), 15.0, Op.is_equal, BIG, Op.mult)
+    ts(pc(10), pc(2), 0.0, Op.is_gt, 4096.0, Op.mult)
+    ts(pc(7), pc(10), 4096.0, Op.add)
+    ts(pc(8), pc(3), 0.0, Op.is_equal)
+    ts(pc(9), pc(3), 16.0, Op.is_equal)
+    ts(A("KC"), A("Ib"), pc(5), Op.mult)
+    ts(A("DC"), A("Ib"), pc(6), Op.mult)
+    ts(A("tm"), A("Dg"), -1.0, Op.is_equal, pc(10), Op.mult)
+    ts(A("tm"), A("tm"), -1.0 / 4096, Op.mult)
+    tt(A("tm"), A("tm"), A("If"), Op.add)
+    ts(A("DM"), A("tm"), 1.0 / 1024, Op.mult)
+    ts(A("DY"), A("tm"), -65.0 / 1024, Op.mult)
+    ts(A("O32f"), A("g32"), pc(1), Op.is_equal)
+    ts(A("O32"), A("g32"), pc(1), Op.is_equal)
+    ts(A("OG"), A("O32"), BIG, Op.mult)
+    ts(A("cy"), A("Dg"), 0.0, Op.is_gt)
+    tt(A("L32"), A("cy"), A("O32"), Op.mult)
+    ts(A("cy"), A("Ib"), -256.0, Op.mult)
+    tt(A("cy"), A("cy"), A("L32"), Op.add)
+    ts(A("LG"), A("cy"), BIG, Op.mult)
+    ts(A("lane96"), A("ln"), pc(1), Op.subtract)
+    ts(A("CT", 1, 50, 5), A("lane96"), -1.0, Op.mult, 95.0, Op.add)
+    ts(A("CT", 2, 50, 5), A("lane96"), -1.0, Op.mult, -1.0, Op.add)
+    for h in range(2):
+        for gg in range(2):
+            ts(A("PF%d%d" % (h, gg)), A("Dg"), 16.0 * (gg - h), Op.is_equal, pc(8 + h), Op.mult)
+            ts(A("PH%d%d" % (h, gg)), A("Dg"), 16.0 * (gg - h), Op.is_equal, pc(8 + h), Op.mult)
+    ts(A("pos0"), A("qq"), pc(0), Op.subtract)
+    ts(A("qrev"), A("pos0"), -1.0, Op.mult, float(L), Op.add)
+    cp(A("wf"), A("wtl"))
+    ts(A("SELW"), A("SEL1"), A("wf"), Op.mult)
+    p8 = slice(0, 8)
+    ts(A("pK", p=p8), A("pI", p=p8), 6, Op.bitwise_and)
+    cp(A("thf", p=p8), A("thl", p=p8))
+    ts(A("pd", 0, 1, p=p8), A("pK", p=p8), 15.0, Op.mult, A("pf", p=p8), Op.add)
+    ts(A("PL", p=p8), A("PL", p=p8), A("pd", 0, 1, p=p8), Op.is_equal)
+    ts(A("ggm"), A("gg"), pc(1), Op.add, A("pf"), Op.is_equal)
+    mm(PS(2, 200, 201), A("PL", p=p8), A("thf", p=p8), True, True)
+    ts(A("thK", 0, 1), PS(2, 200, 201), BIG, Op.add)
+    ts(A("thK", 1, 2), PS(2, 200, 201), BIG, Op.add)
+
+    def spread(j):
+        aff("a", A("thr"), A("ggm"), A("thK", j, j + 1), 0.0)
+        mm(PS(2, 208, 218), A("O32f"), A("thr"), True, True)
+        aff("b", A("thT"), PS(2, 208, 218), 1.0, 0.0)
+
+    spread(0)
+
+    def rows(src, n, i0, i1, tin, tout, dst):
+        ts(A(i0, 0, n), src, 1024.0, Op.mult)
+        ts(A(i1, 0, n), A(i0, 0, n), 10, Op.arith_shift_right)
+        for gg in range(2):
+            ts(A(tin, gg * n // 2, (gg + 1) * n // 2), A(i1, gg, n, 2), -BIG, Op.add)
+        tr(A(tout), A(tin))
+        for a in range(4):
+            dma("YS"[a % 2], dst[2 * a:2 * a + 2, :], A(tout, p=slice(32 * a, 32 * a + n)))
+
+    def distances(lo, hi, last, rec, a, mx, key, copy, b, kv):
+        n = hi - lo
+        per = 512 // n
+        for k0 in range(kv, 16, per):
+            k1 = min(16, k0 + per)
+            for k in range(k0, k1):
+                o = PS(b, n * (k - k0), n * (k - k0) + n)
+                together("P", lambda: [mm(o, A("In"), A(rec, lo, hi), True, False), mm(o, A("Ib"), A(a, 16 * lo + k, 16 * hi, 16), False, True)])
+            act(A(mx, 16 * lo + n * k0, 16 * lo + n * k1), PS(b, 0, n * (k1 - k0)), Fn.Abs)
+            for k in range(k0, k1):
+                mm(PS(key, lo, hi), sel("SEL1", k), A(mx, 16 * lo + n * k, 16 * lo + n * k + n), False, last and kv == 0 and k == 15)
+        for k in range(kv):
+            mm(PS(key, lo, hi), sel("SELN", k), A(a, 16 * lo + k, 16 * hi, 16), False, False)
+        for k in range(kv):
+            m = A(mx, 16 * lo + n * k, 16 * lo + n * k + n)
+            tt(m, A(a, 16 * lo + k, 16 * hi, 16), PS(0, copy + lo, copy + hi), Op.max)
+            mm(PS(key, lo, hi), sel("SEL2", k), m, False, last and k == kv - 1)
+
+    def guests(t):
+        gx, kv = "gx%d" % t, OPT["kv"][t]
+        to_list(PS(2, 224, 234), "SELW", gx, L)
+        ts(A("hi"), PS(2, 224, 234), 77.0 * t, Op.add)
+        ts(A("hj"), A("hi"), W - 1, Op.bitwise_and)
+        cp(A("h16"), A("hj"))
+        gc, ga = "gc16%d" % (t % 2), "ga%d" % (t % 2)
+        cp(A(gc), IND(col, A("h16")))
+        for lo, hi, on in OPT["gcuts"][t]:
+            gather(on, A(ga, 16 * lo, 16 * hi), A("X"), A(gc, lo, hi))
+        mm(PS(4, 0, L), A("BON%d" % kv), A(gx), True, False)
+        if kv:
+            mm(PS(0, 256, 256 + L), A("Ib"), A(gx), True, True)
+        for lo in (0, L // 2):
+            distances(lo, lo + L // 2, lo > 0, gx, ga, "gab", 4, 256, 6, kv)
+        tr(A("gT"), PS(4, 0, L))
+        scan(A("GS%d" % (t % 2)), A("gT"), A("patA"), 2 * BIG, Op.min, Op.add)
+
+    def judge(t):
+        tt(A("gJ"), A("GS%d" % (t % 2), 15, L, 16), A("gm%d" % t, 0, 10), Op.min)
+        for gg in range(2):
+            red(A("JT", gg, gg + 1), A("gJ", gg, 10, 2), Op.max)
+        tr(A("JU"), A("JT"))
+        red(A("rb%d" % t, 3, 4), A("JU"), Op.max)
+        send_all(A("rb%d" % t, 3, 4), "rb%d" % t, "ab%d" % t, "lb%d" % t)
+
+    def guest_rows(t):
+        ts(A("ok"), A("gJ"), 1024.0, Op.mult)
+        ts(A("ol"), A("ok"), 10, Op.arith_shift_right)
+        ts(A("og"), A("ol"), -BIG, Op.add)
+        cp(A("slT"), A("gm%d" % t, 10, 20))
+        swap(2, 32, "PH", "slT", 0, 1)
+        swap(2, 48, "PF", "og", 0, 1)
+        ts(A("sl16"), PS(2, 32, 42), 0.0, Op.add)
+        aff("d", A("mL"), PS(2, 48, 58), 1.0, 0.0)
+        tt(A("mD"), IND(A("mL"), A("jj16", 0, 10)), A("mask", 0, L), Op.mult)
+        cp(IND(A("mw"), A("sl16")), A("mD"))
+        mm(PS(2, 256, 256 + U), A("BOf"), A("mw", 0, U), True, True)
+        aff("f", A("ogT"), PS(2, 256, 256 + U), 1.0, 0.0)
+        dma("S", T.yg[:], A("ogT", p=slice(0, 128, 16)))
+
+    def raise_limits(t):
+        aff("j", A("b1"), A("thK", t - 1, t), 0.25, 0.5 - 1.0 / 1024)
+        red(A("br"), A("rb%d" % t, 3, 3 + N), Op.max)
+        ts(A("b2"), A("br"), 0.25, Op.mult, A("b1"), Op.subtract)
+        name = "thK"
+        if t == NT - 1:
+            name = "tho"
+            ts(A("tho", 0, t), A("thK", 0, t), -BIG, Op.add)
+        ts(A(name, t, t + 1), A("b2"), 0.0, Op.max, A(name, t - 1, t), Op.add)
+
+    def leavers(t):
+        out, n = "lv%d" % (t % 2), 10
+        ts(A("st1"), PS(3, 0, 50, 5), -4.0, Op.mult, BIG, Op.max)
+        tt(A(out, 0, 10), A("mS"), A("st1"), Op.min)
+        if t == NT - 2:
+            n = 20
+            aff("i", A("st3"), PS(3, 0, 50, 5), 1.0 / BIG, 95.5)
+            tt(A("st2"), A("st3"), PS(3, 0, 50, 5), Op.max)
+            tt(A(out, 10, 20), A("st2"), A("lane96"), Op.min)
+        send(A(out, 0, n), A("gm%d" % (t + 1), 0, n), 1 + t % (N - 1), "am%d" % (t + 1), "lm%d" % (t + 1))
+
+    def seeds(dst):
+        ts(A("stmp"), IND(col, A("sd16")), 1.0, Op.add)
+        ts(dst, A("stmp"), W - 1, Op.bitwise_and)
+
+    for t in range(NT):
+        last = t == NT - 1
+        step[0] = t
+        pos, cur = "pos%d" % (t % 2), "cur%d" % (t % 2)
+        ppos, pcur = "pos%d" % ((t + 1) % 2), "cur%d" % ((t + 1) % 2)
+        if t == 0:
+            own, vp = A("Xo", 0, L), "P1"
+            seeds(A("stm2"))
+            cp(A("c16"), A("stm2"))
+            gather("S", own, A("X"), A("od16", 0, 10))
+        else:
+            own, vp = A("own%d" % (t % 2)), "vp"
+            ts(A("off1"), PS(5, 0, 10), float(L), Op.add)
+            cp(A("c16"), IND(A("colx"), A("off1")))
+            aff("e", A("pt"), PS(5, 16, 26), -1.0, A(pcur))
+            ts(A("fl"), PS(5, 16, 26), 0.0, Op.is_lt)
+            tt(A(pos), A("pt"), A(ppos), Op.max)
+            cp(A("off2"), A(pos))
+            gather("S", own, A("Xo", 0, L * (t + 1)), A("off2"))
+            gather("S", A("vp"), A("P1", 0, L * (t + 1)), A("off2"))
+        for lo, hi, on in OPT["cuts"][t]:
+            gather(on, A("a", 16 * lo, 16 * hi), A("X"), A("c16", lo, hi))
+        if 1 <= t < NT - 1:
+            send(own, A("gx%d" % (t + 1)), 1 + t % (N - 1), "ax%d" % (t + 1), "lx%d" % (t + 1))
+        cF, v16 = A("cF%d" % (t % 2)), A("v16%d" % (t % 2))
+        cp(cF, A("c16"))
+        mm(PS(0, 0, L), A("Ib"), own, True, True)
+        mm(PS(1, 0, L), A("KC"), A("ones"), True, False)
+        mm(PS(1, 0, L), A("BON%d" % OPT["ko"][t]), own, False, False)
+        act(A("yy"), cF, Fn.Identity, bias=192.0 - 31.5 / 64, scale=1.0 / 64)
+        mm(PS(1, 0, L), A("Iy"), A("yy"), False, False)
+        if OPT["dd"] == "P":
+            together("P", lambda: [mm(PS(5, 64, 64 + L), A("BO"), A(vp, 0, L), True, False), mm(PS(5, 64, 64 + L), A("If"), cF, False, True)])
+            act(A("ad"), PS(5, 64, 64 + L), Fn.Abs, bias=-2048.0)
+        else:
+            mm(PS(5, 64, 64 + L), A("BO"), A(vp, 0, L), True, True)
+            tt(A("dd"), cF, PS(5, 64, 64 + L), Op.add)
+            act(A("ad"), A("dd"), Fn.Abs, bias=-2048.0)
+        ts(A("pen"), A("ad"), 16.0, Op.is_lt, pc(7), Op.mult)
+        mm(PS(1, 0, L), A("Ib"), A("pen"), False, False)
+        if t >= 1:
+            to_list(PS(2, 176, 186), "SELN", vp, L)
+            ts(v16, PS(2, 176, 186), 2048.0, Op.add)
+        cp(IND(col, A("od16", 0, 10) if t == 0 else v16), cF)
+        if t >= 2:
+            judge(t)
+        if 1 <= t < NT - 1:
+            guests(t + 1)
+        if t >= 3:
+            raise_limits(t - 1)
+        if last:
+            mm(PS(5, 256, 256 + L), A("BO"), A(vp, 0, L), True, True)
+            aff("f", A("ov"), PS(5, 256, 256 + L), -1.0, 2048.0)
+            dma("Y", T.yv[:], A("ov", p=slice(0, 128, 16)))
+            for h in range(2):
+                cp(A("on", 480 * h, 480 * h + 480), IND(col, A("od16", 30 * h, 30 * h + 30)))
+                dma("Y", T.yn[:, 480 * h:480 * h + 480], A("on", 480 * h, 480 * h + 480), 4000.0)
+        else:
+            if t >= 1:
+                mm(PS(2, 192, 202), A("BO"), A("fl"), True, True)
+                red(A("nfr"), PS(2, 192, 202), Op.add)
+                aff("g", A(cur), A("nfr"), 1.0, A(pcur))
+            ts(A("nx16"), A("qrev"), A(cur), Op.add)
+            gather("S", A("nxp"), A("P1", 0, L * (t + 2)), A("nx16"))
+            together("P", lambda: [mm(PS(3, 0, L), A("DC"), A("ones"), True, False), mm(PS(3, 0, L), A("DY"), A("yy"), False, False),
+                                   mm(PS(3, 0, L), A("DM"), cF, False, True)])
+            tr(A("TD"), PS(3, 0, L))
+            mm(PS(3, 0, 50), A("If"), A("CT"), True, False)
+            to_list(PS(2, 240, 250), "SELN", "nxp", L)
+            ts(A("vi"), PS(2, 240, 250), 4095.0, Op.add)
+            ts(A("vj"), A("vi"), W - 1, Op.bitwise_and)
+            cp(A("sd16"), A("vj"))
+            seeds(A("colx", 0, L))
+            gather("S", A("Xo", L * (t + 1), L * (t + 2)), A("X"), A("od16", 10 * (t + 1), 10 * (t + 2)))
+            if t >= 3:
+                spread(t - 1)
+        ch = OPT["chunks"][t]
+        for j in range(len(ch) - 1):
+            distances(ch[j], ch[j + 1], j == len(ch) - 2, own["r"][0][0], "a", "mx", 1, 0, 7, OPT["ko"][t])
+        tr(A("TK"), PS(1, 0, L))
+        scan(A("S", 0, L), A("TK"), A("patA"), 2 * BIG, Op.min, Op.add)
+        SA = A("S", 15, L, 16)
+        tt(A("mS"), SA, A("mOld"), Op.min)
+        if last:
+            rows(A("mS"), 10, "oi", "oj", "om", "omT", T.ym)
+            guest_rows(t)
+            raise_limits(t)
+            for gg in range(2):
+                dma("YS"[gg], T.yt[gg:8:2, :], A("tho", 0, NT, p=slice(gg, 128, 32)))
+            break
+        tt(A("tG"), SA, A("mG"), Op.min)
+        tt(A("tS"), SA, A("nF"), Op.min)
+        tt(A("go"), A("tG"), A("thT"), Op.is_ge)
+        tt(A("fI", 1, 50, 5), A("tS"), A("thT"), Op.is_ge)
+        tt(A("fI", 2, 50, 5), A("mS"), A("thT"), Op.is_ge)
+        mm(PS(3, 0, 50, 5), A("LG"), A("go"), False, False)
+        for s in range(1, 5):
+            mm(PS(3, 10 * s, 50, 5), A("OG"), A("go", 0, 10 - 2 * s), False, False)
+        mm(PS(3, 0, 50), A("L32"), A("fI"), False, False)
+        for s in range(1, 5):
+            mm(PS(3, 10 * s, 50), A("O32"), A("fI", 0, 50 - 10 * s), False, s == 4)
+        scan(A("S", L, 2 * L), A("TK"), A("TD"), 2 * BIG, Op.min, Op.add)
+        aff("h", A("d5", 0, 50, 5), A("fI", 2, 50, 5), 4096.0, -2048.0)
+        tt(A("I20"), A("S", 15, 2 * L, 16), A("mulc"), Op.mult)
+        ts(A("lo20", 0, 10), A("I20", 0, 10), 4032, Op.bitwise_and)
+        ts(A("lo20", 10, 20), A("I20", 10, 20), 63, Op.bitwise_and)
+        tt(A("d5", 3, 50, 5), A("lo20", 0, 10), A("lo20", 10, 20), Op.add)
+        scan(A("s5"), PS(3, 0, 50), A("d5"), -2048.0, Op.max, Op.min)
+        swap(5, 0, "PH", "s5", 3, 5)
+        swap(5, 16, "PH", "s5", 2, 5)
+        ts(A("oPM"), A("s5", 2, 50, 5), 0.5, Op.add, 2.0 ** 17, Op.mult)
+        tt(A("mG"), A("mS"), A("oPM"), Op.min)
+        ts(A("nF"), A("oPM"), -1.0, Op.mult, 4095.0 + BIG, Op.min)
+        tt(A("mOld"), A("mG"), A("nF"), Op.max)
+        if t >= 1:
+            leavers(t)
+
+    if "seq" not in PLAN:
+        PLAN["seq"] = arrange(nodes)
+    emit(PLAN["seq"])

@@ -4,43 +4,46 @@ from concourse.mybir import dt, AluOpType, AxisListType, ActivationFunctionType
 
 W, L, U, NT, Q = 2048, 160, 96, 6, 960
 f32, bf, i32, u16, f16 = "float32", "bfloat16", "int32", "uint16", "float16"
+C0, SD, NX = 8, 2248, 385
 SB = {
-    "X": (W, bf), "colx": (L + W, i32), "odl": (60, i32), "wtl": (1, i32), "thl": (1, i32),
-    "od16": (60, u16), "odf": (60, f32), "jj16": (60, u16), "odD": (320, f32), "ptmp": (320, f32),
-    "P1": (Q, bf), "Xo": (Q, bf), "own0": (L, bf), "own1": (L, bf), "vp": (L, bf), "nxp": (L, bf),
+    "X": (W, bf), "colx": (SD + L, i32), "odl": (60, i32), "wtl": (1, i32), "thl": (1, i32),
+    "od16": (60, u16), "odD": (Q, f16), "ptmp": (Q // 2, f32),
+    "P1": (Q, bf), "own0": (L, bf), "own1": (L, bf), "VW0": (NX + L, bf), "VW1": (NX + L, bf),
     "a": (16 * L, bf), "mx": (16 * L, bf), "ga0": (16 * L, bf), "ga1": (16 * L, bf), "gab": (16 * L, bf),
-    "v160": (10, u16), "v161": (10, u16), "c16": (L, u16), "cF0": (L, f32), "cF1": (L, f32), "dd": (L, f32), "ad": (L, bf), "pen": (L, bf), "yy": (L, bf),
+    "v16": (10, u16), "c16": (L, u16), "cH": (L, f16), "ad": (L, bf), "pen": (L, bf), "yy": (L, bf),
     "TK": (L, f32), "TD": (L, f32), "S": (2 * L, f32), "patA": (L, f32),
-    "fI": (50, bf), "go": (10, bf), "d5": (50, f32), "s5": (50, f16), "I20": (20, i32), "lo20": (20, i32),
-    "mulc": (20, f32), "off1": (10, u16), "off2": (10, u16), "pt": (10, f32), "pos0": (10, f32), "pos1": (10, f32),
-    "cur0": (1, f32), "cur1": (1, f32), "fl": (10, bf), "nfr": (1, f32), "nx16": (10, u16),
-    "vi": (10, i32), "vj": (10, i32), "sd16": (10, u16), "v16": (10, u16), "stmp": (L, i32), "stm2": (L, i32),
+    "fI": (60, bf), "go": (10, bf), "d5": (60, f32), "s5": (60, f16), "Fk": (10, f32),
+    "off1": (10, u16), "off2": (10, u16), "nx0": (10, u16), "nx1": (10, u16), "sd16": (10, u16), "stmp": (L, i32),
     "st1": (10, f32), "st2": (10, f32), "slT": (10, f16), "sl16": (10, u16),
-    "mS": (10, f32), "mG": (10, f32), "mOld": (10, f32), "oPM": (10, f32), "nF": (10, f32),
-    "thT": (10, f32), "thr": (10, f32), "tS": (10, f32), "tG": (10, f32), "tA": (10, f32), "tu": (10, f32), "tv": (10, f32),
-    "mL": (10, f32), "mD": (L, f32), "mw": (256, f32), "lv0": (20, f32), "lv1": (20, f32), "st3": (10, f32), "gJ": (10, f32),
-    "hi": (10, i32), "hj": (10, i32), "h16": (10, u16), "gc160": (L, u16), "gc161": (L, u16), "gT": (L, f32), "GS0": (L, f32), "GS1": (L, f32), "BON0": (128, bf), "BON6": (128, bf),
-    "JT": (32, f32), "JU": (32, f32), "br": (1, f32), "b1": (1, f32), "b2": (1, i32), "b3": (1, i32),
-    "thK": (8, f32), "tho": (8, f32), "thf": (1, f32), "wf": (1, f32),
-    "oi": (10, i32), "oj": (10, i32), "ok": (10, i32), "ol": (10, i32), "om": (32, f32), "omT": (32, f32), "og": (10, f32), "ogT": (U, f32),
-    "ov": (L, f32), "on": (Q, f32),
-    "pI": (1, i32), "pJ": (4, i32), "pK": (1, i32), "pf": (1, f32), "pc": (12, f32), "pd": (2, f32),
-    "Dg": (128, f32), "g16": (128, f32), "g32": (128, f32),
-    "xs1": (144, f32), "xm16": (320, f32), "ln": (10, f32), "qq": (10, f32), "gg": (10, f32), "jjI": (60, i32),
+    "mS": (10, f32), "mOld": (10, f32), "fr": (10, bf), "un": (10, bf), "thr": (30, f32),
+    "gJ": (10, f32), "mZ": (L, f32), "mT": (L, f32), "mw": (2 * L, f32), "gw": (U, f32), "gZ": (L, f32), "gY": (L, f32),
+    "hi": (10, i32), "hj": (10, i32), "gc0": (L, u16), "gc1": (L, u16), "gT": (L, f32), "GS0": (L, f32), "GS1": (L, f32),
+    "JT": (32, f32), "JU": (32, f32), "br": (1, f32), "b2": (1, i32),
+    "thK": (8, f32), "tho": (8, f32), "thf": (1, f32), "wf": (1, f32), "oi": (10, i32), "ov": (L, f32), "on": (Q, f32),
+    "pI": (1, i32), "pJ": (4, i32), "pK": (1, i32), "pf": (1, f32), "pc": (16, f32), "pd": (2, f32),
+    "Dg": (128, bf), "g16": (128, bf), "g32": (128, bf),
+    "xs1": (144, bf), "xm16": (128, bf), "ln": (10, f32), "qq": (10, f32), "gg": (30, f32),
     "SEL1": (144, bf), "SEL2": (144, bf), "SELN": (144, bf), "SELW": (144, bf),
-    "BO": (128, bf), "BON16": (128, bf), "BON4": (128, bf), "BON8": (128, bf), "BON10": (128, bf), "BON12": (128, bf), "BON14": (128, bf), "BOf": (128, f32), "Ib": (128, bf), "In": (128, bf), "Iy": (128, bf), "If": (128, f32),
-    "KC": (128, bf), "DC": (128, bf), "DM": (128, f32), "DY": (128, bf), "ones": (L, bf), "cy": (128, bf), "cn": (128, bf), "onef": (128, f32),
-    "L32": (128, bf), "O32": (128, bf), "O32f": (128, f32), "LG": (128, bf), "OG": (128, bf), "tm": (128, f32), "tn": (128, f32),
-    "PL": (128, f32), "mask": (320, f32), "mBIG": (L, f32), "lane96": (10, f32), "qrev": (10, f32), "ggm": (10, f32), "CT": (50, f32),
+    "BO": (128, bf), "BOh": (128, f16), "Ib": (128, bf), "In": (128, bf), "Iy": (128, bf), "If": (128, f32), "Ih": (128, f16),
+    "IB": (128, bf), "NF0": (128, bf), "NF1": (128, bf),
+    "KC": (128, f16), "DC": (128, f16), "DM": (128, f16), "DY": (128, bf), "ones": (L, bf), "oneH": (L, f16),
+    "L32": (128, bf), "O32": (128, bf), "O32f": (128, f32), "LG": (128, bf), "OG": (128, bf),
+    "tm": (128, bf), "tn": (128, bf), "tk": (128, bf), "tl": (128, bf),
+    "PL": (128, f32), "mask": (16, f32), "lanec": (10, f32), "ggm": (30, f32), "CT": (60, f32),
 }
+for _k in range(0, 17, 2):
+    SB["BON%d" % _k] = (128, bf)
 for _h in range(2):
     for _g in range(2):
         SB["PH%d%d" % (_h, _g)] = (128, f16)
-        SB["PF%d%d" % (_h, _g)] = (128, f32)
+        SB["PB%d%d" % (_h, _g)] = (128, f16)
 for _t in range(2, NT):
     SB["gx%d" % _t] = (L, bf)
-    SB["gm%d" % _t] = (20, f32)
-    SB["rb%d" % _t] = (12, f32)
+    SB["gm%d" % _t] = (12, f32)
+    SB["lv%d" % _t] = (12, f32)
+    SB["dm%d" % _t] = (12, f32)
+    SB["h%d" % _t] = (10, u16)
+    SB["rb%d" % _t] = (20, f32)
 PLACE, FILL = {}, {}
 for _k, (_n, _d) in SB.items():
     if _n > 320:
@@ -55,15 +58,17 @@ for _b in range(8):
     SCRATCH["ps%d" % _b] = ("psum", [128, 512], f32)
 NDMA = 30
 SEMAPHORES = ["sV", "sS", "sP", "sG"] + ["d%d" % k for k in range(NDMA)] \
-    + ["%s%d" % (n, t) for n in ("ax", "am", "ab", "lx", "lm", "lb") for t in range(2, NT)]
+    + ["%s%d" % (n, t) for n in ("ax", "am", "ab", "lx", "lm", "lb") for t in range(2, NT)] + ["ag", "lg"]
 BYTES = {f32: 4, bf: 2, i32: 4, u16: 2, f16: 2}
-OPT = {"cuts": [[(0, 40, "S"), (40, 80, "V"), (80, 130, "S"), (130, 160, "V")], [(0, 40, "S"), (40, 80, "V"), (80, 120, "S"), (120, 160, "S")]]
-       + [[(0, 40, "S"), (40, 64, "V"), (64, 80, "S"), (80, 120, "S"), (120, 160, "S")]] * 3
-       + [[(0, 40, "S"), (40, 80, "S"), (80, 120, "S"), (120, 160, "S")]],
-       "chunks": [[0, 80, 160]] * 6, "gcuts": [[(0, 40, "S"), (40, 80, "S"), (80, 120, "S"), (120, 160, "S")]] * 6,
-       "kv": [0, 0, 10, 10, 10, 10], "ko": [14, 14, 12, 12, 12, 16],
-       "seed": 1, "noise": 0.5, "rounds": 30, "moves": 1300, "slack": 300.0, "onS": "abdegij", "dd": "P",
-       "wake": 120.0, "far": 3500.0, "fan": 6500.0, "gather": 1.56, "scatter": 3.8}
+CYC = 0.83
+OPT = {
+    "cuts": [[(0, 44, "S"), (44, 80, "V"), (80, 124, "S"), (124, 160, "V")], [(0, 40, "S"), (40, 80, "V"), (80, 130, "S"), (130, 160, "V")]]
+    + [[(0, 80, "S"), (80, 160, "S")]] * 4,
+    "chunks": [[0, 80, 160]] * 6, "ko": [12, 16, 16, 16, 16, 12],
+    "gcuts": [[(0, 40, "S"), (40, 80, "S"), (80, 120, "S"), (120, 160, "S")]] * 6, "gchunks": [[0, 160]] * 6, "kv": [0, 0, 16, 16, 16, 16],
+    "back": [5], "fans": [[2], [3], [4], [5]], "out": [0, 20, 40, 60],
+    "seed": 1, "moves": 1500, "slack": 0.004, "turn": 0.1, "tol": [600.0, 40.0, 0.5], "far": 2800.0, "fan": 5000.0, "first": 2000.0,
+    "cases": [(1.1, 1.56, 3.8, 15.0, 110.0, 1.0), (1.0, 1.2, 2.5, 0.0, 80.0, 0.7), (1.3, 1.8, 5.0, 30.0, 130.0, 1.3)], "scale": [1.0, 0.9, 1.25]}
 PLAN = {}
 
 
@@ -75,120 +80,120 @@ def arrange(nodes):
         x[0] = (x[0] * 1103515245 + 12345) % 2147483648
         return x[0] / 2147483648.0
     qs = [nd["q"] for nd in nodes]
-    pred = [[(d, 0.0 if qs[d] == nd["q"] == "P" else OPT["wake"]) for d in nd["deps"]] for nd in nodes]
+    pred = [[(d, 0 if qs[d] == nd["q"] == "P" or qs[d] is None else 1) for d in nd["deps"]] for nd in nodes]
     succ = [[] for nd in nodes]
     for i in range(n):
         for d, w in pred[i]:
             succ[d].append((i, w))
-
-    wake = OPT["wake"]
     banks = [([r[0] for it in nd["items"] for r in it["reads"] + it["writes"] if r[0] not in SB] + [None])[0] for nd in nodes]
+    cases = []
+    for f, gat, sca, fix, wake, far in OPT["cases"]:
+        cases.append(([f * (nd["dur"][0] + gat * nd["dur"][1] + sca * nd["dur"][2]) + fix * nd["dur"][3] for nd in nodes],
+                      [nd["lat"] * (far if nd["far"] else 1.0) for nd in nodes], wake))
 
-    def first(slots, t):
-        lo, hi = 0, len(slots)
-        while lo < hi:
-            mid = (lo + hi) // 2
-            if slots[mid][1] <= t:
-                lo = mid + 1
-            else:
-                hi = mid
-        return lo
-
-    def place(prio, back, noise):
-        start, end, busy = [0.0] * n, [0.0] * n, {}
-        for i in sorted(range(n), key=lambda j: (-prio[j], -j if back else j)):
-            dur, lat = nodes[i]["dur"], nodes[i]["lat"]
-            if noise:
-                dur *= 1 + noise * (2 * rnd() - 1)
-            t = max([end[d] + w for d, w in (succ if back else pred)[i]] + [0.0]) + (lat if back else 0.0)
+    def play(seq, case):
+        dur, lat, wake = case
+        end, free, used = [0.0] * n, {}, {}
+        for i in seq:
+            t = free.get(qs[i], 0.0)
+            for d, w in pred[i]:
+                if end[d] + w * wake > t:
+                    t = end[d] + w * wake
+            b = banks[i]
+            if b:
+                u = used.setdefault(b, {})
+                for q in u:
+                    if q != qs[i] and u[q] + wake > t:
+                        t = u[q] + wake
+                u[qs[i]] = t + dur[i]
             if qs[i]:
-                slots, b = busy.setdefault(qs[i], []), banks[i]
-                while True:
-                    lo = first(slots, t)
-                    while lo < len(slots) and slots[lo][0] < t + dur:
-                        t = max(t, slots[lo][1])
-                        lo += 1
-                    if b is None:
-                        break
-                    uses, was = busy.setdefault(b, []), t
-                    k = first(uses, t - wake)
-                    while k < len(uses) and uses[k][0] < t + dur + wake:
-                        if uses[k][2] != qs[i]:
-                            t = max(t, uses[k][1] + wake)
-                        k += 1
-                    if t == was:
-                        uses.insert(first(uses, t), (t, t + dur, qs[i]))
-                        break
-                slots.insert(lo, (t, t + dur))
-            start[i], end[i] = t, t + dur + (0.0 if back else lat)
-        return start, end
+                free[qs[i]] = t + dur[i]
+            end[i] = t + dur[i] + lat[i]
+        return max(end)
 
-    level = [0.0] * n
-    for i in range(n - 1, -1, -1):
-        level[i] = nodes[i]["dur"] + nodes[i]["lat"] + max([level[j] + w for j, w in succ[i]] + [0.0])
-    best = place(level, False, 0.0)
-    for it in range(OPT["rounds"]):
-        now = place(place(best[1], True, OPT["noise"])[1], False, 0.0)
-        if max(now[1]) <= max(best[1]) + OPT["slack"] * (1 - it / OPT["rounds"]):
-            best = now
-    marks = [i for i in range(n) if qs[i] is None]
+    def deal(way, back, case, tol):
+        dur, lat, wake = case
+        before, after = (succ, pred) if back else (pred, succ)
+        left = [len(p) for p in before]
+        ready, end, seq = [0.0] * n, [0.0] * n, []
+        pool, free, used = {q: [] for q in (None, "V", "S", "P", "G", "Y")}, {q: 0.0 for q in "VSPGY"}, {}
+        for i in range(n):
+            if not left[i]:
+                ready[i] = lat[i] if back else 0.0
+                pool[qs[i]].append(i)
+        while len(seq) < n:
+            if pool[None]:
+                i = pool[None].pop()
+                t = ready[i]
+            else:
+                now, q, at = 1e18, None, None
+                for q2 in "VSPGY":
+                    if pool[q2] and free[q2] < now:
+                        a2 = []
+                        for j in pool[q2]:
+                            t = ready[j] if ready[j] > free[q2] else free[q2]
+                            if banks[j] in used:
+                                for q3, e in used[banks[j]].items():
+                                    if q3 != q2 and e + wake > t:
+                                        t = e + wake
+                            a2.append((t, j))
+                        t2 = min(a2)[0]
+                        if t2 < now:
+                            now, q, at = t2, q2, a2
+                near = [(way[j], t, j) for t, j in at if t <= now + tol[0]]
+                w, t, i = max(near)
+                if t > now:
+                    fits = [e for e in near if e[1] < t and e[1] + dur[e[2]] <= t + tol[1] + tol[2] * (t - e[1])]
+                    if fits:
+                        w, t, i = max(fits)
+                pool[q].remove(i)
+                free[q] = t + dur[i]
+                if banks[i]:
+                    used.setdefault(banks[i], {})[q] = t + dur[i]
+            end[i] = t + dur[i] + (0.0 if back else lat[i])
+            seq.append(i)
+            for j, w in after[i]:
+                ready[j] = max(ready[j], end[i] + w * wake + (lat[j] if back else 0.0))
+                left[j] -= 1
+                if not left[j]:
+                    pool[qs[j]].append(j)
+        return seq, end
+
+    def score(seq):
+        return sum(play(seq, c) / s for c, s in zip(cases, OPT["scale"]))
+
     kinds = {}
     for i in range(n):
-        if qs[i] and nodes[i]["items"][0]["writes"]:
-            kinds.setdefault((qs[i], nodes[i]["items"][0]["writes"][0][0], nodes[i]["step"]), []).append(i)
+        w = nodes[i]["items"][0]["writes"] if nodes[i]["items"] else []
+        kinds.setdefault((qs[i], w[0][0] if w else "", nodes[i]["step"]), []).append(i)
     kinds = list(kinds.values())
-    kind = {i: k for k in range(len(kinds)) for i in kinds[k]}
-    seen = [None, None]
-
-    def score(p):
-        return max(p[1]) + 0.3 * sum(p[1][i] for i in marks) / len(marks)
-
-    top = best
+    dur, lat, wake = cases[0]
+    way = [0.0] * n
+    for i in range(n - 1, -1, -1):
+        way[i] = dur[i] + lat[i] + max([way[j] + w * wake for j, w in succ[i]] + [0.0])
+    tol = list(OPT["tol"])
+    seq, end = deal(way, False, cases[0], tol)
+    best = top = (score(seq), seq, way, end, tol)
     for it in range(OPT["moves"]):
-        key = list(best[0])
-        if seen[0] is not best:
-            ends = {(qs[i], round(best[0][i] + nodes[i]["dur"])): i for i in range(n) if qs[i]}
-            pairs, i = [], max(range(n), key=lambda j: best[1][j])
-            while i is not None:
-                d = max(pred[i], key=lambda e: best[1][e[0]] + e[1]) if pred[i] else None
-                if d is not None and best[1][d[0]] + d[1] + 1 >= best[0][i]:
-                    i = d[0]
-                else:
-                    j = ends.get((qs[i], round(best[0][i])))
-                    if j is not None and kind.get(j) != kind.get(i):
-                        pairs.append((j, i))
-                    i = j
-            seen[0], seen[1] = best, pairs
-        if seen[1] and rnd() < 0.75:
-            j, i = seen[1][int(rnd() * len(seen[1]))]
-            by = 3000.0 * rnd() * rnd() + 100
-            way = rnd()
-            if way < 0.6 and j in kind:
-                s = 1 if way < 0.3 else -2
-                for e in kinds[kind[j]]:
-                    key[e] += s * by
-            elif i in kind:
-                for e in kinds[kind[i]]:
-                    key[e] -= by
+        way, tol = list(best[2]), list(best[4])
+        r = rnd()
+        if r < OPT["turn"]:
+            way = deal(best[3], True, cases[0], tol)[1]
+        elif r < OPT["turn"] + 0.05:
+            tol = [a * (0.6 + 0.8 * rnd()) for a in OPT["tol"]]
         else:
-            by = (rnd() - 0.65) * 6000.0 * rnd()
-            for i in kinds[int(rnd() * len(kinds))]:
-                key[i] += by
-        for i in range(n - 1, -1, -1):
-            for j, w in succ[i]:
-                if key[i] >= key[j]:
-                    key[i] = key[j] - 1.0
-        now = place([-k for k in key], False, 0.0)
-        if it % 8 == 7:
-            now = place(place(now[1], True, 0.2)[1], False, 0.0)
-        if score(now) <= score(best) + OPT["slack"] * (1 - it / OPT["moves"]) * rnd():
+            for _ in range(1 + int(3 * rnd())):
+                by = (rnd() - 0.5) * 5000.0 * rnd()
+                for i in kinds[int(rnd() * len(kinds))]:
+                    way[i] += by
+        seq, end = deal(way, False, cases[0], tol)
+        now = (score(seq), seq, way, end, tol)
+        if now[0] <= best[0] * (1 + OPT["slack"] * (1 - it / OPT["moves"]) * rnd()):
             best = now
-            if score(now) < score(top):
+            if now[0] < top[0]:
                 top = now
-    start, end = top
-    PLAN["times"] = (start, end)
-    PLAN["nodes"] = nodes
-    return sorted(range(n), key=lambda j: (start[j], j))
+    PLAN["times"] = [round(play(top[1], c)) for c in cases]
+    return top[1]
 
 
 def rank_program(g, core, T, topo):
@@ -200,7 +205,7 @@ def rank_program(g, core, T, topo):
     QU = {"V": g.vector, "S": g.scalar, "P": g.tensor, "G": g, "Y": g.sync}
     size = {k: n for k, (n, d) in SB.items()}
     size.update({"ps%d" % b: 512 for b in range(8)})
-    nodes, macro, group, ndma, step = [], [], {}, [0], [-1]
+    nodes, macro, group, opened, ndma, step = [], [], {}, {}, [0], [-1]
     nwr = {k: np.full(n, -1) for k, n in size.items()}
     nrd = {k: [] for k in size}
 
@@ -225,6 +230,17 @@ def rank_program(g, core, T, topo):
         reads = [r for it in items for r in it["reads"]]
         writes = [r for it in items for r in it["writes"]]
         me, deps = len(nodes), set(after)
+        if q == "P":
+            st = opened.setdefault(writes[0][0], {"stop": -1, "whole": []})
+            if acc in (None, "start"):
+                deps.add(st["stop"])
+            if acc is None:
+                st["whole"].append(me)
+            elif acc == "start":
+                deps.update(st["whole"])
+                st["whole"] = []
+            elif acc == "stop":
+                st["stop"] = me
         if acc in ("mid", "stop"):
             name = writes[0][0]
             deps.update(group[name]["ops"] if acc == "stop" else group[name]["ops"][:1])
@@ -247,7 +263,7 @@ def rank_program(g, core, T, topo):
             nrd[name] = [(o, s2) for o, s2 in nrd[name] if o == me or not mark[s2].all()]
         deps.discard(-1)
         deps.discard(me)
-        nodes.append({"q": q, "items": items, "dur": dur, "lat": lat, "deps": sorted(deps), "step": step[0]})
+        nodes.append({"q": q, "items": items, "dur": dur, "lat": lat, "deps": sorted(deps), "step": step[0], "far": False})
         return me
 
     def call(q, fn, out, ins, per=None, acc=None):
@@ -257,30 +273,30 @@ def rank_program(g, core, T, topo):
             reads += x["r"] + x.get("x", [])
         n = max(out["n"], ins[0]["n"] if ins else 0)
         if q == "P":
-            dur = max(64, out["n"]) * (0.5 if ins[0]["two"] else 2.0)
+            dur = [max(64, out["n"]) * CYC / 2 * (1.0 if ins[0]["two"] else 4.0), 0, 0, 0]
         elif q == "G":
-            dur = 150.0 + 2 * n
+            dur = [140.0 + 2 * n * CYC, 0, 0, 0]
         elif "x" in out:
-            dur = 50.0 + out["n"] * OPT["scatter"]
+            dur = [50.0, 0, out["n"] * CYC, 0]
         elif ins and "x" in ins[0]:
-            dur = 60.0 + out["n"] * OPT["gather"]
+            dur = [50.0 if q == "V" else 65.0, out["n"] * CYC, 0, 0]
         elif q == "S":
-            dur = 65.0 + n
+            dur = [65.0 + n * CYC, 0, 0, 0]
         else:
-            dur = max(64.0, n * (per or (0.5 if all(x["two"] or x["n"] == 1 for x in [out] + ins) else 1.0)))
+            dur = [CYC * max(64.0, n * (per or (0.5 if all(x["two"] or x["n"] == 1 for x in [out] + ins) else 1.0))), 0, 0, 1]
         it = {"kind": "c", "q": q, "fn": fn, "reads": reads, "writes": writes}
         if macro:
             macro[0].append(it)
-            macro[1] += dur
+            macro[1] = [a + b for a, b in zip(macro[1], dur)]
         else:
             node(q, [it], dur, acc=acc)
 
-    def together(q, body):
-        macro.extend([[], 0.0])
+    def together(q, body, acc=None):
+        macro.extend([[], [0, 0, 0, 0]])
         body()
         items, dur = macro
         del macro[:]
-        node(q, items, dur)
+        node(q, items, dur, acc=acc)
 
     def emit(seq):
         cnt = {"V": 0, "S": 0, "P": 0, "G": 0}
@@ -372,14 +388,11 @@ def rank_program(g, core, T, topo):
     def tr(out, in_):
         call("V", lambda: g.vector.transpose(out["ap"], in_["ap"]), out, [in_])
 
+    def mset(out, c):
+        call("V", lambda: g.vector.memset(out["ap"], c), out, [])
+
     def act(out, in_, fn, bias=0.0, scale=1.0):
         call("S", lambda: g.scalar.activation(out["ap"], in_["ap"], fn, bias=ap(bias), scale=ap(scale)), out, [in_, bias, scale])
-
-    def aff(tag, out, in_, scale, bias):
-        if tag in OPT["onS"]:
-            act(out, in_, Fn.Identity, bias, scale)
-        else:
-            ts(out, in_, scale, Op.mult, bias, Op.add)
 
     def gather(on, out, win, off):
         x = IND(win, off)
@@ -401,8 +414,8 @@ def rank_program(g, core, T, topo):
     def fill(out, c):
         iota(out, [[0, out["n"]]], c, 0)
 
-    def diag(out, in_):
-        call("G", lambda: g.affine_select(out["ap"], in_["ap"], [[-1, 128]], Op.is_equal, 0.0, 0, 1), out, [in_])
+    def lower(out, in_):
+        call("G", lambda: g.affine_select(out["ap"], in_["ap"], [[1, 128]], Op.is_gt, 0.0, 0, -1), out, [in_])
 
     def dma(q, out, in_, lat=2500.0):
         sem = "d%d" % ndma[0]
@@ -410,11 +423,13 @@ def rank_program(g, core, T, topo):
         reads = [wide(r) for r in in_["r"]] if isinstance(in_, dict) else []
         writes = [wide(r) for r in out["r"]] if isinstance(out, dict) else []
         node(q, [{"kind": "d", "q": q, "sem": sem, "c": 16, "reads": reads, "writes": writes,
-                  "fn": lambda: QU[q].dma_start(ap(out), ap(in_)).then_inc(T.sem[sem], 16)}], 100.0, lat)
+                  "fn": lambda: QU[q].dma_start(ap(out), ap(in_)).then_inc(T.sem[sem], 16)}], [60.0, 0, 0, 0], lat)
 
     def remote(fn, src, lsem, nl, dst, rsem, nr, lat):
-        me = node("G", [{"kind": "r", "q": "G", "sem": lsem, "c": nl, "reads": [wide(r) for r in src["r"]], "writes": [], "fn": fn}], 1000.0, lat)
-        node(None, [{"kind": "in", "q": None, "sem": rsem, "c": nr, "reads": [], "writes": dst["r"]}], 1.0, 0.0, after=[me])
+        me = node("G", [{"kind": "r", "q": "G", "sem": lsem, "c": nl, "reads": [wide(r) for r in src["r"]], "writes": [], "fn": fn}],
+                  [900.0, 0, 0, 0], lat + (0.0 if any(nd["far"] for nd in nodes) else OPT["first"]))
+        nodes[me]["far"] = True
+        node(None, [{"kind": "in", "q": None, "sem": rsem, "c": nr, "reads": [], "writes": dst["r"]}], [1.0, 0, 0, 0], 200.0, after=[me])
 
     def bits(m):
         return bin(m).count("1")
@@ -438,16 +453,16 @@ def rank_program(g, core, T, topo):
             plan.append((near, sum(1 << e for e in es)))
         return plan
 
-    def send_all(src, name, rsem, lsem):
-        trs, tot = [], 0
+    def send_all(name, w, rsem, lsem):
+        src, trs, tot = A(name, 4 - w, 4), [], 0
         for dsts, m in fan_plan(core):
             js = [(T.rank_of(x) - rank - 1) % N for x in dsts]
             trs.append(RemoteDMATransfer(dst_ids=[DstId(rid=topo.addr(x)[0], pnc=topo.addr(x)[1]) for x in dsts],
                                          dma_engine_mask=m, remote_sem=T.sem[rsem], src=src["ap"],
-                                         dsts=[A(name, 4 + j, 5 + j)["ap"] for j in js]))
+                                         dsts=[A(name, 4 + w * j, 4 + w * j + w)["ap"] for j in js]))
             tot += bits(m)
         got = sum(bits(m) for x in T.cores if x != core for dsts, m in fan_plan(x) if core in dsts)
-        remote(lambda: g.remote_dma_fused(trs, local_sem=T.sem[lsem]), src, lsem, tot, A(name, 4, 3 + N), rsem, got, OPT["fan"])
+        remote(lambda: g.remote_dma_fused(trs, local_sem=T.sem[lsem]), src, lsem, tot, A(name, 4, 4 + w * (N - 1)), rsem, got, OPT["fan"])
 
     def PS(b, a, e, s=1):
         return A("ps%d" % b, a, e, s)
@@ -458,117 +473,104 @@ def rank_program(g, core, T, topo):
     def pc(j):
         return A("pc", j, j + 1)
 
-    def to_list(out, name, src, n):
-        together("P", lambda: [mm(out, sel(name, r), A(src, r, n, 16), r == 0, r == 15) for r in range(16)])
+    def to_list(out, name, src, a):
+        together("P", lambda: [mm(out, sel(name, r), A(src, a + r, a + L, 16), r == 0, r == 15) for r in range(16)])
 
-    def swap(b, a, kind, src, e, stride):
+    def swap(b, a, src, stride, parts):
+        ways = [(kind, e, gg) for kind, e in parts for gg in range(2)]
         together("P", lambda: [mm(PS(b, a + h, a + 10, 2), A("%s%d%d" % (kind, h, gg)), A(src, stride * gg + e, 10 * stride, 2 * stride),
-                                  gg == 0, gg == 1) for h in range(2) for gg in range(2)])
+                                  j == 0, j == len(ways) - 1) for h in range(2) for j, (kind, e, gg) in enumerate(ways)])
 
-    col = A("colx", L, L + W)
-    BIG = 8192.0
+    col = A("colx", C0, C0 + W)
+    BIG = 8179.75
+    HALF = BIG + 0.5 - 1.0 / 32
+    TH0 = BIG + 2.0 - 1.0 / 32
+    R16, R1 = 1.5 * 2 ** 19, 1.5 * 2 ** 23
 
     dma("S", A("odl"), T.od[:])
-    dma("Y", col, T.nb[:], 7000.0)
-    dma("Y", A("X"), T.xs[:], 9500.0)
+    dma("Y", col, T.nb[:], 7500.0)
+    dma("Y", A("X"), T.xs[:], 10000.0)
     nodes[-2]["items"] += nodes[-1]["items"]
-    nodes[-1].update({"q": None, "items": [], "dur": 2500.0, "lat": 0.0, "deps": [len(nodes) - 2]})
+    nodes[-1].update({"q": None, "items": [], "dur": [0, 0, 0, 0], "lat": 2700.0, "deps": [len(nodes) - 2]})
     dma("S", A("thl", p=slice(0, 8)), T.th[:])
     dma("S", A("wtl"), T.wt[:])
 
     iota(A("pI"), [[0, 1]], 0, 1)
     iota(A("pf"), [[0, 1]], 0, 1)
-    iota(A("jjI"), [[1, 60]], 0, 0)
-    iota(A("xm16"), [[0, 20], [1, 16]], 0, 0)
+    iota(A("xm16"), [[0, 8], [1, 16]], 0, 0)
     iota(A("g16"), [[16, 8], [0, 16]], 0, 0)
     iota(A("Dg"), [[1, 128]], 0, -1)
     iota(A("xs1"), [[1, 144]], -15, 0)
     iota(A("g32"), [[32, 4], [0, 32]], 0, 0)
-    iota(A("ln"), [[32, 5], [0, 2]], U, 1)
-    iota(A("qq"), [[16, 10]], 0, 1)
-    iota(A("gg"), [[0, 5], [1, 2]], 0, 0)
+    iota(A("ln"), [[32, 5], [0, 2]], 0, 1)
+    iota(A("qq"), [[16, 10]], L, 1)
+    iota(A("gg"), [[0, 15], [1, 2]], 0, 0)
     iota(A("PL"), [[1, 128]], 0, 0)
-    fill(A("ones"), 1)
-    fill(A("onef"), 1)
-    fill(A("cn"), -1)
-    diag(A("Ib"), A("ones", 0, 128))
-    diag(A("If"), A("onef"))
-    diag(A("In"), A("cn"))
-    fill(A("patA"), 0)
-    fill(A("patA", 15, L, 16), int(BIG))
-    fill(A("CT"), -2048)
-    fill(A("CT", 0, 50, 5), int(160.5 * BIG))
-    fill(A("fI"), 0)
-    fill(A("d5"), 2048)
-    fill(A("d5", 4, 50, 5), -2048)
-    fill(A("mulc", 0, 10), 65536)
-    fill(A("mulc", 10, 20), 1024)
-    fill(A("cur0"), L - 1)
-    fill(A("nF"), 4095 + int(BIG))
-    fill(A("mG"), -65536)
-    fill(A("mOld"), 4095 + int(BIG))
-    for name in ("mw", "JT", "om") + (("BON0",) if 0 in OPT["kv"][2:] else ()):
-        fill(A(name), 0)
+    for name, a, b, c in (("colx", 0, C0, 0), ("colx", C0 + W, SD, 0), ("VW0", L, NX, 0), ("VW1", L, NX, 0), ("ones", 0, L, 1),
+                          ("patA", 0, L, 0), ("fI", 0, 60, 0), ("d5", 0, 60, 0), ("CT", 0, 60, 1), ("fr", 0, 10, 32768),
+                          ("mOld", 0, 10, 32768), ("JT", 0, 32, 0), ("mZ", 0, L, 0), ("gZ", 0, L, 0), ("mw", 0, 2 * L, 0)):
+        fill(A(name, a, b), c)
+    mset(A("patA", 15, L, 16), BIG)
+    mset(A("d5", 5, 60, 6), 1.0)
+    for ch, c in ((0, -416.5 * 32768), (1, NX / 1024), (2, (NX + U) / 1024), (4, 352.0 / 1024)):
+        mset(A("CT", ch, 60, 6), c)
     for j, m in enumerate((112, 96, 15, 16)):
         ts(A("pJ", j, j + 1), A("pI"), m, Op.bitwise_and)
     cp(A("pc", 0, 4), A("pJ"))
-    cp(A("jj16"), A("jjI"))
-    ts(A("mask"), A("xm16"), pc(2), Op.is_equal)
+    ts(A("mask"), A("xm16", 0, 16), pc(2), Op.is_equal)
     ts(pc(4), pc(2), -128.0, Op.mult)
-    ts(A("BOf"), A("g16"), pc(0), Op.is_equal)
-    cp(A("odf"), A("odl"))
+    ts(A("BOh"), A("g16"), pc(0), Op.is_equal)
     cp(A("od16"), A("odl"))
-
-    def table(j):
-        tt(A("odD"), IND(A("odf"), A("jj16", 20 * j, 20 * j + 20)), A("mask"), Op.mult)
-        mm(PS(6 + j % 2, 0, 320), A("BOf"), A("odD"), True, True)
-        act(A("ptmp"), PS(6 + j % 2, 0, 320), Fn.Relu, bias=pc(4))
-        act(A("P1", 320 * j, 320 * j + 320), A("ptmp"), Fn.Relu, bias=128.0, scale=-1.0)
-
-    for j in range(3):
-        table(j)
-    ts(A("vi"), A("odl", 0, 10), 2047.0, Op.add)
-    ts(A("vj"), A("vi"), 2047, Op.bitwise_and)
-    cp(A("sd16"), A("vj"))
+    for r in range(16):
+        ts(A("odD", r, Q, 16), A("odl"), A("mask", r, r + 1), Op.mult)
+    for j in range(2):
+        mm(PS(6 + j, 0, 480), A("BOh"), A("odD", 480 * j, 480 * j + 480), True, True)
+        act(A("ptmp"), PS(6 + j, 0, 480), Fn.Relu, bias=pc(4))
+        act(A("P1", 480 * j, 480 * j + 480), A("ptmp"), Fn.Relu, bias=128.0, scale=-1.0)
+    act(A("VW0", 0, L), A("P1", 0, L), Fn.Copy)
+    act(A("VW0", NX, NX + L), A("P1", L, 2 * L), Fn.Copy)
+    ts(A("sd16"), A("odl", 0, 10), C0 - 1.0, Op.add)
+    ts(A("If"), A("Dg"), 0.0, Op.is_equal)
+    for name, c in (("Ib", 1.0), ("In", -1.0), ("Ih", 1.0), ("Iy", 1.0 / 512), ("IB", 32768.0)):
+        ts(A(name), A("Dg"), 0.0, Op.is_equal, c, Op.mult)
+    cp(A("oneH"), A("ones"))
     ts(A("BO"), A("g16"), pc(0), Op.is_equal)
     ts(A("BON16"), A("g16"), pc(0), Op.is_equal, -1.0, Op.mult)
-    for kv in sorted(set(OPT["kv"][2:] + OPT["ko"]) - {0, 16}):
+    for kv in sorted(set(OPT["kv"][2:] + OPT["ko"]) - {16}):
         ts(A("tn"), A("xm16", 0, 128), float(kv), Op.is_lt)
         tt(A("BON%d" % kv), A("tn"), A("BON16"), Op.mult)
     ts(A("SEL2"), A("xs1"), pc(0), Op.is_equal, 2.0, Op.mult)
     ts(A("SELN"), A("xs1"), pc(0), Op.is_equal, -1.0, Op.mult)
     ts(A("SEL1"), A("xs1"), pc(0), Op.is_equal)
-    ts(A("Iy"), A("Ib"), 1.0 / 1024, Op.mult)
-    ts(pc(5), pc(2), -3.0, Op.add, 1.0 / 16, Op.mult)
-    ts(pc(6), pc(2), 15.0, Op.is_equal, BIG, Op.mult)
-    ts(pc(10), pc(2), 0.0, Op.is_gt, 4096.0, Op.mult)
-    ts(pc(7), pc(10), 4096.0, Op.add)
-    ts(pc(8), pc(3), 0.0, Op.is_equal)
-    ts(pc(9), pc(3), 16.0, Op.is_equal)
+    ts(pc(5), pc(2), 1.0 / 16, Op.mult, -415.0 / 1024, Op.add)
+    ts(pc(6), pc(2), 15.0, Op.is_equal, 8192.0, Op.mult)
+    ts(pc(10), pc(2), 0.0, Op.is_gt, -1.0, Op.mult)
+    ts(pc(7), pc(10), -4096.0, Op.mult, 4096.0, Op.add)
+    for h in range(2):
+        ts(pc(8 + h), pc(3), 16.0 * h, Op.is_equal, 1024.0, Op.mult)
+        ts(pc(12 + h), pc(3), 16.0 * h, Op.is_equal, 32768.0, Op.mult)
+        ts(A("tn"), A("g16"), pc(1), Op.subtract, 16.0 * h, Op.is_equal)
+        ts(A("NF%d" % h), A("tn"), 1.0 / 32768, Op.mult)
     ts(A("KC"), A("Ib"), pc(5), Op.mult)
     ts(A("DC"), A("Ib"), pc(6), Op.mult)
     ts(A("tm"), A("Dg"), -1.0, Op.is_equal, pc(10), Op.mult)
-    ts(A("tm"), A("tm"), -1.0 / 4096, Op.mult)
-    tt(A("tm"), A("tm"), A("If"), Op.add)
+    tt(A("tm"), A("tm"), A("Ib"), Op.add)
     ts(A("DM"), A("tm"), 1.0 / 1024, Op.mult)
-    ts(A("DY"), A("tm"), -65.0 / 1024, Op.mult)
+    ts(A("DY"), A("tm"), -66.0 / 1024, Op.mult)
     ts(A("O32f"), A("g32"), pc(1), Op.is_equal)
-    ts(A("O32"), A("g32"), pc(1), Op.is_equal)
-    ts(A("OG"), A("O32"), BIG, Op.mult)
-    ts(A("cy"), A("Dg"), 0.0, Op.is_gt)
-    tt(A("L32"), A("cy"), A("O32"), Op.mult)
-    ts(A("cy"), A("Ib"), -256.0, Op.mult)
-    tt(A("cy"), A("cy"), A("L32"), Op.add)
-    ts(A("LG"), A("cy"), BIG, Op.mult)
-    ts(A("lane96"), A("ln"), pc(1), Op.subtract)
-    ts(A("CT", 1, 50, 5), A("lane96"), -1.0, Op.mult, 95.0, Op.add)
-    ts(A("CT", 2, 50, 5), A("lane96"), -1.0, Op.mult, -1.0, Op.add)
+    ts(A("O32"), A("g32"), pc(1), Op.is_equal, 1.0 / 1024, Op.mult)
+    ts(A("OG"), A("g32"), pc(1), Op.is_equal, -32768.0, Op.mult)
+    lower(A("L32"), A("O32"))
+    lower(A("tl"), A("OG"))
+    ts(A("tk"), A("Dg"), 0.0, Op.is_equal, 512.0 * 32768, Op.mult)
+    tt(A("LG"), A("tl"), A("tk"), Op.add)
+    ts(A("d5", 2, 60, 6), A("ln"), pc(1), Op.subtract, 1.0 / 1024, Op.mult)
+    ts(A("lanec"), A("ln"), pc(1), Op.subtract, 672.0, Op.add)
     for h in range(2):
         for gg in range(2):
-            ts(A("PF%d%d" % (h, gg)), A("Dg"), 16.0 * (gg - h), Op.is_equal, pc(8 + h), Op.mult)
             ts(A("PH%d%d" % (h, gg)), A("Dg"), 16.0 * (gg - h), Op.is_equal, pc(8 + h), Op.mult)
-    ts(A("pos0"), A("qq"), pc(0), Op.subtract)
-    ts(A("qrev"), A("pos0"), -1.0, Op.mult, float(L), Op.add)
+            ts(A("PB%d%d" % (h, gg)), A("Dg"), 16.0 * (gg - h), Op.is_equal, pc(12 + h), Op.mult)
+    ts(A("nx0"), A("qq"), pc(0), Op.subtract)
     cp(A("wf"), A("wtl"))
     ts(A("SELW"), A("SEL1"), A("wf"), Op.mult)
     p8 = slice(0, 8)
@@ -578,24 +580,19 @@ def rank_program(g, core, T, topo):
     ts(A("PL", p=p8), A("PL", p=p8), A("pd", 0, 1, p=p8), Op.is_equal)
     ts(A("ggm"), A("gg"), pc(1), Op.add, A("pf"), Op.is_equal)
     mm(PS(2, 200, 201), A("PL", p=p8), A("thf", p=p8), True, True)
-    ts(A("thK", 0, 1), PS(2, 200, 201), BIG, Op.add)
-    ts(A("thK", 1, 2), PS(2, 200, 201), BIG, Op.add)
+    ts(A("thK", 0, 1), PS(2, 200, 201), TH0, Op.add)
+    ts(A("thK", 1, 2), PS(2, 200, 201), TH0, Op.add)
 
-    def spread(j):
-        aff("a", A("thr"), A("ggm"), A("thK", j, j + 1), 0.0)
-        mm(PS(2, 208, 218), A("O32f"), A("thr"), True, True)
-        aff("b", A("thT"), PS(2, 208, 218), 1.0, 0.0)
-
-    spread(0)
-
-    def rows(src, n, i0, i1, tin, tout, dst):
-        ts(A(i0, 0, n), src, 1024.0, Op.mult)
-        ts(A(i1, 0, n), A(i0, 0, n), 10, Op.arith_shift_right)
-        for gg in range(2):
-            ts(A(tin, gg * n // 2, (gg + 1) * n // 2), A(i1, gg, n, 2), -BIG, Op.add)
-        tr(A(tout), A(tin))
-        for a in range(4):
-            dma("YS"[a % 2], dst[2 * a:2 * a + 2, :], A(tout, p=slice(32 * a, 32 * a + n)))
+    def limits(t):
+        if t == 0 or t >= 3:
+            act(A("thr"), A("ggm"), Fn.Identity, bias=-1.0 / 16, scale=A("thK", max(t - 1, 0), max(t - 1, 0) + 1))
+        more = [(442, "IB", A("un")), (452, "IB", A("un")), (462, "IB", A("un"))] if t >= 3 else []
+        if t >= 3:
+            mm(PS(5, 432, 442), A("O32f"), A("thr", 0, 10), True, True)
+            tt(A("un"), A("mOld"), PS(5, 432, 442), Op.is_lt)
+        more += [(452, "Ib", A("fr")), (462, "In", A("fr")), (462, "IB", A("ones", 0, 10))]
+        together("P", lambda: [mm(PS(5, 442, 472), A("O32f"), A("thr"), True, False)]
+                 + [mm(PS(5, a, a + 10), A(w), x, False, j == len(more) - 1) for j, (a, w, x) in enumerate(more)])
 
     def distances(lo, hi, last, rec, a, mx, key, copy, b, kv):
         n = hi - lo
@@ -608,193 +605,183 @@ def rank_program(g, core, T, topo):
             act(A(mx, 16 * lo + n * k0, 16 * lo + n * k1), PS(b, 0, n * (k1 - k0)), Fn.Abs)
             for k in range(k0, k1):
                 mm(PS(key, lo, hi), sel("SEL1", k), A(mx, 16 * lo + n * k, 16 * lo + n * k + n), False, last and kv == 0 and k == 15)
-        for k in range(kv):
-            mm(PS(key, lo, hi), sel("SELN", k), A(a, 16 * lo + k, 16 * hi, 16), False, False)
+        for k0 in range(0, kv, 4):
+            together("P", lambda: [mm(PS(key, lo, hi), sel("SELN", k), A(a, 16 * lo + k, 16 * hi, 16), False, False)
+                                   for k in range(k0, min(kv, k0 + 4))], "mid")
         for k in range(kv):
             m = A(mx, 16 * lo + n * k, 16 * lo + n * k + n)
             tt(m, A(a, 16 * lo + k, 16 * hi, 16), PS(0, copy + lo, copy + hi), Op.max)
             mm(PS(key, lo, hi), sel("SEL2", k), m, False, last and k == kv - 1)
 
-    def guests(t):
-        gx, kv = "gx%d" % t, OPT["kv"][t]
-        to_list(PS(2, 224, 234), "SELW", gx, L)
+    def hop(t):
+        return 1 + (t - 1) % (N - 1)
+
+    def places(t):
+        to_list(PS(2, 224, 234), "SELW", "gx%d" % t, 0)
         ts(A("hi"), PS(2, 224, 234), 77.0 * t, Op.add)
         ts(A("hj"), A("hi"), W - 1, Op.bitwise_and)
-        cp(A("h16"), A("hj"))
-        gc, ga = "gc16%d" % (t % 2), "ga%d" % (t % 2)
-        cp(A(gc), IND(col, A("h16")))
+        cp(A("h%d" % t), A("hj"))
+
+    def guests(t):
+        gx, kv, gc, ga = "gx%d" % t, OPT["kv"][t], "gc%d" % (t % 2), "ga%d" % (t % 2)
+        cp(A(gc), IND(col, A("h%d" % t)))
         for lo, hi, on in OPT["gcuts"][t]:
             gather(on, A(ga, 16 * lo, 16 * hi), A("X"), A(gc, lo, hi))
         mm(PS(4, 0, L), A("BON%d" % kv), A(gx), True, False)
-        if kv:
-            mm(PS(0, 256, 256 + L), A("Ib"), A(gx), True, True)
-        for lo in (0, L // 2):
-            distances(lo, lo + L // 2, lo > 0, gx, ga, "gab", 4, 256, 6, kv)
+        mm(PS(0, 256, 256 + L), A("Ib"), A(gx), True, True)
+        ch = OPT["gchunks"][t]
+        for j in range(len(ch) - 1):
+            distances(ch[j], ch[j + 1], j == len(ch) - 2, gx, ga, "gab", 4, 256, 6, kv)
         tr(A("gT"), PS(4, 0, L))
         scan(A("GS%d" % (t % 2)), A("gT"), A("patA"), 2 * BIG, Op.min, Op.add)
+        if t in OPT["back"]:
+            cp(A("dm%d" % t, 0, 10), A("GS%d" % (t % 2), 15, L, 16))
+            send(A("dm%d" % t, 0, 10), A("gm%d" % t, 0, 10), -hop(t), "am%d" % t, "lm%d" % t)
 
     def judge(t):
-        tt(A("gJ"), A("GS%d" % (t % 2), 15, L, 16), A("gm%d" % t, 0, 10), Op.min)
+        fan = [f for f in OPT["fans"] if t in f][0]
+        mine = A("lv%d" % t, 0, 10) if t in OPT["back"] else A("GS%d" % (t % 2), 15, L, 16)
+        tt(A("gJ"), mine, A("gm%d" % t, 0, 10), Op.min)
         for gg in range(2):
             red(A("JT", gg, gg + 1), A("gJ", gg, 10, 2), Op.max)
         tr(A("JU"), A("JT"))
-        red(A("rb%d" % t, 3, 4), A("JU"), Op.max)
-        send_all(A("rb%d" % t, 3, 4), "rb%d" % t, "ab%d" % t, "lb%d" % t)
-
-    def guest_rows(t):
-        ts(A("ok"), A("gJ"), 1024.0, Op.mult)
-        ts(A("ol"), A("ok"), 10, Op.arith_shift_right)
-        ts(A("og"), A("ol"), -BIG, Op.add)
-        cp(A("slT"), A("gm%d" % t, 10, 20))
-        swap(2, 32, "PH", "slT", 0, 1)
-        swap(2, 48, "PF", "og", 0, 1)
-        ts(A("sl16"), PS(2, 32, 42), 0.0, Op.add)
-        aff("d", A("mL"), PS(2, 48, 58), 1.0, 0.0)
-        tt(A("mD"), IND(A("mL"), A("jj16", 0, 10)), A("mask", 0, L), Op.mult)
-        cp(IND(A("mw"), A("sl16")), A("mD"))
-        mm(PS(2, 256, 256 + U), A("BOf"), A("mw", 0, U), True, True)
-        aff("f", A("ogT"), PS(2, 256, 256 + U), 1.0, 0.0)
-        dma("S", T.yg[:], A("ogT", p=slice(0, 128, 16)))
+        e = 4 - len(fan) + fan.index(t)
+        red(A("rb%d" % fan[-1], e, e + 1), A("JU"), Op.max)
+        if t == fan[-1]:
+            send_all("rb%d" % t, len(fan), "ab%d" % t, "lb%d" % t)
 
     def raise_limits(t):
-        aff("j", A("b1"), A("thK", t - 1, t), 0.25, 0.5 - 1.0 / 1024)
-        red(A("br"), A("rb%d" % t, 3, 3 + N), Op.max)
-        ts(A("b2"), A("br"), 0.25, Op.mult, A("b1"), Op.subtract)
+        fan = [f for f in OPT["fans"] if t in f][0]
+        w = len(fan)
+        red(A("br"), A("rb%d" % fan[-1], 4 - w + fan.index(t), 4 + w * (N - 1), w), Op.max)
+        ts(A("b2"), A("br"), A("thK", t - 1, t), Op.subtract, 0.25, Op.mult)
         name = "thK"
         if t == NT - 1:
             name = "tho"
-            ts(A("tho", 0, t), A("thK", 0, t), -BIG, Op.add)
+            ts(A("tho", 0, t), A("thK", 0, t), -TH0, Op.add)
         ts(A(name, t, t + 1), A("b2"), 0.0, Op.max, A(name, t - 1, t), Op.add)
 
-    def leavers(t):
-        out, n = "lv%d" % (t % 2), 10
-        ts(A("st1"), PS(3, 0, 50, 5), -4.0, Op.mult, BIG, Op.max)
-        tt(A(out, 0, 10), A("mS"), A("st1"), Op.min)
-        if t == NT - 2:
-            n = 20
-            aff("i", A("st3"), PS(3, 0, 50, 5), 1.0 / BIG, 95.5)
-            tt(A("st2"), A("st3"), PS(3, 0, 50, 5), Op.max)
-            tt(A(out, 10, 20), A("st2"), A("lane96"), Op.min)
-        send(A(out, 0, n), A("gm%d" % (t + 1), 0, n), 1 + t % (N - 1), "am%d" % (t + 1), "lm%d" % (t + 1))
+    def guest_rows(t):
+        ts(A("gZ", 15, L, 16), A("gJ"), -HALF, Op.add, R1, Op.add)
+        tr(A("gY"), A("gZ"))
+        ts(IND(A("mw"), A("sl16")), A("gY"), 1.0, Op.mult, -R1, Op.add)
+        send(A("mw", 0, U), A("gw"), hop(t), "ag", "lg")
+        dma("S", T.yg[:], A("gw", p=slice(15, 128, 16)))
 
-    def seeds(dst):
-        ts(A("stmp"), IND(col, A("sd16")), 1.0, Op.add)
-        ts(dst, A("stmp"), W - 1, Op.bitwise_and)
+    def leavers(t):
+        tt(A("lv%d" % (t + 1), 0, 10), A("mS"), PS(3, 0, 60, 6), Op.min)
+        if t + 1 not in OPT["back"]:
+            send(A("lv%d" % (t + 1), 0, 10), A("gm%d" % (t + 1), 0, 10), hop(t + 1), "am%d" % (t + 1), "lm%d" % (t + 1))
+        if t == NT - 2:
+            ts(A("st1"), PS(3, 0, 60, 6), -1.0 / 32768, Op.mult, 95.5, Op.add)
+            tt(A("st2"), A("lanec"), A("st1"), Op.subtract)
+            tt(A("slT"), A("st1"), A("st2"), Op.min)
+            swap(2, 32, "slT", 1, [("PH", 0)])
+            ts(A("sl16"), PS(2, 32, 42), 1.0 / 1024, Op.mult)
+
+    def seeds():
+        cp(A("colx", C0 - 1, C0), A("colx", C0 + W - 1, C0 + W))
+        ts(A("stmp"), IND(A("colx", 0, C0 + W), A("sd16")), 1.0, Op.add)
+        ts(A("colx", SD, SD + L), A("stmp"), W - 1, Op.bitwise_and)
 
     for t in range(NT):
         last = t == NT - 1
         step[0] = t
-        pos, cur = "pos%d" % (t % 2), "cur%d" % (t % 2)
-        ppos, pcur = "pos%d" % ((t + 1) % 2), "cur%d" % ((t + 1) % 2)
+        own, vw = A("own%d" % (t % 2)), "VW%d" % (t % 2)
         if t == 0:
-            own, vp = A("Xo", 0, L), "P1"
-            seeds(A("stm2"))
-            cp(A("c16"), A("stm2"))
-            gather("S", own, A("X"), A("od16", 0, 10))
+            seeds()
+            cp(A("c16"), A("colx", SD, SD + L))
+            v16 = A("od16", 0, 10)
         else:
-            own, vp = A("own%d" % (t % 2)), "vp"
-            ts(A("off1"), PS(5, 0, 10), float(L), Op.add)
+            ts(A("off1"), PS(5, 0, 10), C0 - 9409.0, Op.add)
             cp(A("c16"), IND(A("colx"), A("off1")))
-            aff("e", A("pt"), PS(5, 16, 26), -1.0, A(pcur))
-            ts(A("fl"), PS(5, 16, 26), 0.0, Op.is_lt)
-            tt(A(pos), A("pt"), A(ppos), Op.max)
-            cp(A("off2"), A(pos))
-            gather("S", own, A("Xo", 0, L * (t + 1)), A("off2"))
-            gather("S", A("vp"), A("P1", 0, L * (t + 1)), A("off2"))
+            cp(A("off2"), PS(2, 0, 10))
+            gather("S", A(vw, 0, L), A("VW%d" % ((t - 1) % 2)), A("off2"))
+            to_list(PS(2, 176, 186), "SELN", vw, 0)
+            v16 = A("v16")
+            ts(v16, PS(2, 176, 186), 2048.0, Op.add)
+        gather("S", own, A("X"), v16)
         for lo, hi, on in OPT["cuts"][t]:
             gather(on, A("a", 16 * lo, 16 * hi), A("X"), A("c16", lo, hi))
-        if 1 <= t < NT - 1:
-            send(own, A("gx%d" % (t + 1)), 1 + t % (N - 1), "ax%d" % (t + 1), "lx%d" % (t + 1))
-        cF, v16 = A("cF%d" % (t % 2)), A("v16%d" % (t % 2))
-        cp(cF, A("c16"))
+        if t < NT - 2:
+            send(own, A("gx%d" % (t + 2)), hop(t + 2), "ax%d" % (t + 2), "lx%d" % (t + 2))
+        cp(A("cH"), A("c16"))
+        ts(A("yy"), A("c16"), 1.0 / 64, Op.mult, 192.0 - 31.5 / 64, Op.add)
         mm(PS(0, 0, L), A("Ib"), own, True, True)
-        mm(PS(1, 0, L), A("KC"), A("ones"), True, False)
+        mm(PS(1, 0, L), A("KC"), A("oneH"), True, False)
         mm(PS(1, 0, L), A("BON%d" % OPT["ko"][t]), own, False, False)
-        act(A("yy"), cF, Fn.Identity, bias=192.0 - 31.5 / 64, scale=1.0 / 64)
         mm(PS(1, 0, L), A("Iy"), A("yy"), False, False)
-        if OPT["dd"] == "P":
-            together("P", lambda: [mm(PS(5, 64, 64 + L), A("BO"), A(vp, 0, L), True, False), mm(PS(5, 64, 64 + L), A("If"), cF, False, True)])
-            act(A("ad"), PS(5, 64, 64 + L), Fn.Abs, bias=-2048.0)
-        else:
-            mm(PS(5, 64, 64 + L), A("BO"), A(vp, 0, L), True, True)
-            tt(A("dd"), cF, PS(5, 64, 64 + L), Op.add)
-            act(A("ad"), A("dd"), Fn.Abs, bias=-2048.0)
+        together("P", lambda: [mm(PS(5, 64, 64 + L), A("BO"), A(vw, 0, L), True, False), mm(PS(5, 64, 64 + L), A("Ih"), A("cH"), False, True)])
+        act(A("ad"), PS(5, 64, 64 + L), Fn.Abs, bias=-2048.0)
         ts(A("pen"), A("ad"), 16.0, Op.is_lt, pc(7), Op.mult)
         mm(PS(1, 0, L), A("Ib"), A("pen"), False, False)
-        if t >= 1:
-            to_list(PS(2, 176, 186), "SELN", vp, L)
-            ts(v16, PS(2, 176, 186), 2048.0, Op.add)
-        cp(IND(col, A("od16", 0, 10) if t == 0 else v16), cF)
+        cp(IND(col, v16), A("c16"))
         if t >= 2:
             judge(t)
         if 1 <= t < NT - 1:
             guests(t + 1)
-        if t >= 3:
-            raise_limits(t - 1)
+        if t < NT - 2:
+            places(t + 2)
         if last:
-            mm(PS(5, 256, 256 + L), A("BO"), A(vp, 0, L), True, True)
-            aff("f", A("ov"), PS(5, 256, 256 + L), -1.0, 2048.0)
+            guest_rows(t)
+            mm(PS(5, 256, 256 + L), A("BO"), A(vw, 0, L), True, True)
+            act(A("ov"), PS(5, 256, 256 + L), Fn.Identity, bias=2048.0, scale=-1.0)
             dma("Y", T.yv[:], A("ov", p=slice(0, 128, 16)))
-            for h in range(2):
-                cp(A("on", 480 * h, 480 * h + 480), IND(col, A("od16", 30 * h, 30 * h + 30)))
-                dma("Y", T.yn[:, 480 * h:480 * h + 480], A("on", 480 * h, 480 * h + 480), 4000.0)
+            for a, b in zip(OPT["out"], OPT["out"][1:]):
+                cp(A("on", 16 * a, 16 * b), IND(col, A("od16", a, b)))
+                dma("Y", T.yn[:, 16 * a:16 * b], A("on", 16 * a, 16 * b), 2200.0 + 40.0 * b)
         else:
             if t >= 1:
-                mm(PS(2, 192, 202), A("BO"), A("fl"), True, True)
-                red(A("nfr"), PS(2, 192, 202), Op.add)
-                aff("g", A(cur), A("nfr"), 1.0, A(pcur))
-            ts(A("nx16"), A("qrev"), A(cur), Op.add)
-            gather("S", A("nxp"), A("P1", 0, L * (t + 2)), A("nx16"))
-            together("P", lambda: [mm(PS(3, 0, L), A("DC"), A("ones"), True, False), mm(PS(3, 0, L), A("DY"), A("yy"), False, False),
-                                   mm(PS(3, 0, L), A("DM"), cF, False, True)])
+                together("P", lambda: [mm(PS(2, 192, 193), A("NF%d" % (j % 2)), A("fr", j, j + 1), j == 0, j == 9) for j in range(10)])
+                ts(A("nx%d" % (t % 2)), A("nx%d" % ((t - 1) % 2)), PS(2, 192, 193), Op.add)
+                gather("S", A(vw, NX, NX + L), A("P1", 0, L * (t + 2)), A("nx%d" % (t % 2)))
+            together("P", lambda: [mm(PS(3, 0, L), A("DC"), A("oneH"), True, False), mm(PS(3, 0, L), A("DY"), A("yy"), False, False),
+                                   mm(PS(3, 0, L), A("DM"), A("cH"), False, True)])
             tr(A("TD"), PS(3, 0, L))
-            mm(PS(3, 0, 50), A("If"), A("CT"), True, False)
-            to_list(PS(2, 240, 250), "SELN", "nxp", L)
-            ts(A("vi"), PS(2, 240, 250), 4095.0, Op.add)
-            ts(A("vj"), A("vi"), W - 1, Op.bitwise_and)
-            cp(A("sd16"), A("vj"))
-            seeds(A("colx", 0, L))
-            gather("S", A("Xo", L * (t + 1), L * (t + 2)), A("X"), A("od16", 10 * (t + 1), 10 * (t + 2)))
+            mm(PS(3, 0, 60), A("If"), A("CT"), True, False)
+            to_list(PS(2, 240, 250), "SELN", vw, NX)
+            ts(A("sd16"), PS(2, 240, 250), 2048.0 + C0 - 1, Op.add)
+            seeds()
             if t >= 3:
-                spread(t - 1)
+                raise_limits(t - 1)
+            limits(t)
         ch = OPT["chunks"][t]
         for j in range(len(ch) - 1):
             distances(ch[j], ch[j + 1], j == len(ch) - 2, own["r"][0][0], "a", "mx", 1, 0, 7, OPT["ko"][t])
         tr(A("TK"), PS(1, 0, L))
         scan(A("S", 0, L), A("TK"), A("patA"), 2 * BIG, Op.min, Op.add)
         SA = A("S", 15, L, 16)
-        tt(A("mS"), SA, A("mOld"), Op.min)
         if last:
-            rows(A("mS"), 10, "oi", "oj", "om", "omT", T.ym)
-            guest_rows(t)
+            tt(A("mS"), SA, A("mOld"), Op.min)
+            ts(A("oi"), A("mS"), -HALF, Op.add, 4095.0, Op.min)
+            cp(A("mZ", 15, L, 16), A("oi"))
+            tr(A("mT"), A("mZ"))
+            dma("S", T.ym[:], A("mT", p=slice(15, 128, 16)))
+            raise_limits(t - 1)
             raise_limits(t)
             for gg in range(2):
                 dma("YS"[gg], T.yt[gg:8:2, :], A("tho", 0, NT, p=slice(gg, 128, 32)))
             break
-        tt(A("tG"), SA, A("mG"), Op.min)
-        tt(A("tS"), SA, A("nF"), Op.min)
-        tt(A("go"), A("tG"), A("thT"), Op.is_ge)
-        tt(A("fI", 1, 50, 5), A("tS"), A("thT"), Op.is_ge)
-        tt(A("fI", 2, 50, 5), A("mS"), A("thT"), Op.is_ge)
-        mm(PS(3, 0, 50, 5), A("LG"), A("go"), False, False)
+        tt(A("go"), SA, PS(5, 452, 462), Op.is_ge)
+        tt(A("fI", 1, 60, 6), SA, PS(5, 462, 472), Op.is_lt)
+        tt(A("fI", 2, 60, 6), SA, PS(5, 442, 452), Op.is_lt)
+        tt(A("d5", 0, 60, 6), SA, PS(5, 442, 452), Op.is_lt)
+        mm(PS(3, 0, 60, 6), A("LG"), A("go"), False, False)
         for s in range(1, 5):
-            mm(PS(3, 10 * s, 50, 5), A("OG"), A("go", 0, 10 - 2 * s), False, False)
-        mm(PS(3, 0, 50), A("L32"), A("fI"), False, False)
+            mm(PS(3, 12 * s, 60, 6), A("OG"), A("go", 0, 10 - 2 * s), False, False)
+        mm(PS(3, 0, 60), A("L32"), A("fI"), False, False)
         for s in range(1, 5):
-            mm(PS(3, 10 * s, 50), A("O32"), A("fI", 0, 50 - 10 * s), False, s == 4)
+            mm(PS(3, 12 * s, 60), A("O32"), A("fI", 0, 60 - 12 * s), False, s == 4)
         scan(A("S", L, 2 * L), A("TK"), A("TD"), 2 * BIG, Op.min, Op.add)
-        aff("h", A("d5", 0, 50, 5), A("fI", 2, 50, 5), 4096.0, -2048.0)
-        tt(A("I20"), A("S", 15, 2 * L, 16), A("mulc"), Op.mult)
-        ts(A("lo20", 0, 10), A("I20", 0, 10), 4032, Op.bitwise_and)
-        ts(A("lo20", 10, 20), A("I20", 10, 20), 63, Op.bitwise_and)
-        tt(A("d5", 3, 50, 5), A("lo20", 0, 10), A("lo20", 10, 20), Op.add)
-        scan(A("s5"), PS(3, 0, 50), A("d5"), -2048.0, Op.max, Op.min)
-        swap(5, 0, "PH", "s5", 3, 5)
-        swap(5, 16, "PH", "s5", 2, 5)
-        ts(A("oPM"), A("s5", 2, 50, 5), 0.5, Op.add, 2.0 ** 17, Op.mult)
-        tt(A("mG"), A("mS"), A("oPM"), Op.min)
-        ts(A("nF"), A("oPM"), -1.0, Op.mult, 4095.0 + BIG, Op.min)
-        tt(A("mOld"), A("mG"), A("nF"), Op.max)
+        ts(A("Fk"), SA, R16, Op.add, -R16 - 320.0 / 1024, Op.add)
+        tt(A("d5", 4, 60, 6), SA, A("Fk"), Op.subtract)
+        tt(A("d5", 3, 60, 6), A("S", L + 15, 2 * L, 16), A("Fk"), Op.subtract)
+        scan(A("s5"), PS(3, 0, 60), A("d5"), 1.0, Op.min, Op.max)
+        swap(5, 0, "s5", 6, [("PH", 3), ("PB", 4)])
+        swap(2, 0, "s5", 6, [("PH", 2)])
+        tt(A("mS"), SA, A("mOld"), Op.min)
+        ts(A("fr"), A("s5", 2, 60, 6), 0.25, Op.is_gt, 32768.0, Op.mult)
+        tt(A("mOld"), A("mS"), A("fr"), Op.max)
         if t >= 1:
             leavers(t)
 

import numpy as np
from concourse.bass import DstId, RemoteDMATransfer
from concourse.mybir import dt, AluOpType, AxisListType, ActivationFunctionType

W, L, U, NT, Q = 2048, 160, 96, 6, 960
f32, bf, i32, u16, f16 = "float32", "bfloat16", "int32", "uint16", "float16"
C0, SD, NX = 8, 2248, 385
SB = {
    "X": (W, bf), "colx": (SD + L, i32), "odl": (60, i32), "wtl": (1, i32), "thl": (1, i32),
    "od16": (60, u16), "odD": (Q, f16), "ptmp": (Q // 2, f32),
    "P1": (Q, bf), "own0": (L, bf), "own1": (L, bf), "VW0": (NX + L, bf), "VW1": (NX + L, bf),
    "a": (16 * L, bf), "mx": (16 * L, bf), "ga0": (16 * L, bf), "ga1": (16 * L, bf), "gab": (16 * L, bf),
    "v16": (10, u16), "c16": (L, u16), "cH": (L, f16), "ad": (L, bf), "pen": (L, bf), "yy": (L, bf),
    "TK": (L, f32), "TD": (L, f32), "S": (2 * L, f32), "patA": (L, f32),
    "fI": (60, bf), "go": (10, bf), "d5": (60, f32), "s5": (60, f16), "Fk": (10, f32),
    "off1": (10, u16), "off2": (10, u16), "nx0": (10, u16), "nx1": (10, u16), "sd16": (10, u16), "stmp": (L, i32),
    "st1": (10, f32), "st2": (10, f32), "slT": (10, f16), "sl16": (10, u16),
    "mS": (10, f32), "mOld": (10, f32), "fr": (10, bf), "un": (10, bf), "thr": (30, f32),
    "gJ": (10, f32), "mZ": (L, f32), "mT": (L, f32), "mw": (2 * L, f32), "gw": (U, f32), "gZ": (L, f32), "gY": (L, f32),
    "hi": (10, i32), "hj": (10, i32), "gc0": (L, u16), "gc1": (L, u16), "gT": (L, f32), "GS0": (L, f32), "GS1": (L, f32),
    "JT": (32, f32), "JU": (32, f32), "br": (1, f32), "b2": (1, i32),
    "thK": (8, f32), "tho": (8, f32), "thf": (1, f32), "wf": (1, f32), "oi": (10, i32), "ov": (L, f32), "on": (Q, f32),
    "pI": (1, i32), "pJ": (4, i32), "pK": (1, i32), "pf": (1, f32), "pc": (16, f32), "pd": (2, f32),
    "Dg": (128, bf), "g16": (128, bf), "g32": (128, bf),
    "xs1": (144, bf), "xm16": (128, bf), "ln": (10, f32), "qq": (10, f32), "gg": (30, f32),
    "SEL1": (144, bf), "SEL2": (144, bf), "SELN": (144, bf), "SELW": (144, bf),
    "BO": (128, bf), "BOh": (128, f16), "Ib": (128, bf), "In": (128, bf), "Iy": (128, bf), "If": (128, f32), "Ih": (128, f16),
    "IB": (128, bf), "NF0": (128, bf), "NF1": (128, bf),
    "KC": (128, f16), "DC": (128, f16), "DM": (128, f16), "DY": (128, bf), "ones": (L, bf), "oneH": (L, f16),
    "L32": (128, bf), "O32": (128, bf), "O32f": (128, f32), "LG": (128, bf), "OG": (128, bf),
    "tm": (128, bf), "tn": (128, bf), "tk": (128, bf), "tl": (128, bf),
    "PL": (128, f32), "mask": (16, f32), "lanec": (10, f32), "ggm": (30, f32), "CT": (60, f32),
}
for _k in range(0, 17, 2):
    SB["BON%d" % _k] = (128, bf)
for _h in range(2):
    for _g in range(2):
        SB["PH%d%d" % (_h, _g)] = (128, f16)
        SB["PB%d%d" % (_h, _g)] = (128, f16)
for _t in range(2, NT):
    SB["gx%d" % _t] = (L, bf)
    SB["gm%d" % _t] = (12, f32)
    SB["lv%d" % _t] = (12, f32)
    SB["dm%d" % _t] = (12, f32)
    SB["h%d" % _t] = (10, u16)
    SB["rb%d" % _t] = (20, f32)
PLACE, FILL = {}, {}
for _k, (_n, _d) in SB.items():
    if _n > 320:
        PLACE[_k] = (_k, 0)
    else:
        PLACE[_k] = ("m_" + _d, FILL.get(_d, 0))
        FILL[_d] = FILL.get(_d, 0) + -(-_n // 16) * 16
SCRATCH = {k: ("sbuf", [128, n], d) for k, (n, d) in SB.items() if n > 320}
for _d, _n in FILL.items():
    SCRATCH["m_" + _d] = ("sbuf", [128, _n], _d)
for _b in range(8):
    SCRATCH["ps%d" % _b] = ("psum", [128, 512], f32)
NDMA = 30
SEMAPHORES = ["sV", "sS", "sP", "sG"] + ["d%d" % k for k in range(NDMA)] \
    + ["%s%d" % (n, t) for n in ("ax", "am", "ab", "lx", "lm", "lb") for t in range(2, NT)] + ["ag", "lg"]
BYTES = {f32: 4, bf: 2, i32: 4, u16: 2, f16: 2}
CYC = 0.83
OPT = {
    "cuts": [[(0, 44, "S"), (44, 80, "V"), (80, 124, "S"), (124, 160, "V")], [(0, 40, "S"), (40, 80, "V"), (80, 130, "S"), (130, 160, "V")]]
    + [[(0, 80, "S"), (80, 160, "S")]] * 4,
    "chunks": [[0, 80, 160]] * 6, "ko": [12, 16, 16, 16, 16, 12],
    "gcuts": [[(0, 40, "S"), (40, 80, "S"), (80, 120, "S"), (120, 160, "S")]] * 6, "gchunks": [[0, 160]] * 6, "kv": [0, 0, 16, 16, 16, 16],
    "back": [5], "fans": [[2], [3], [4], [5]], "out": [0, 20, 40, 60],
    "seed": 1, "moves": 1500, "slack": 0.004, "turn": 0.1, "tol": [600.0, 40.0, 0.5], "far": 2800.0, "fan": 5000.0, "first": 2000.0,
    "cases": [(1.1, 1.56, 3.8, 15.0, 110.0, 1.0), (1.0, 1.2, 2.5, 0.0, 80.0, 0.7), (1.3, 1.8, 5.0, 30.0, 130.0, 1.3)], "scale": [1.0, 0.9, 1.25]}
PLAN = {}


def arrange(nodes):
    n = len(nodes)
    x = [OPT["seed"] * 7919 + 1]

    def rnd():
        x[0] = (x[0] * 1103515245 + 12345) % 2147483648
        return x[0] / 2147483648.0
    qs = [nd["q"] for nd in nodes]
    pred = [[(d, 0 if qs[d] == nd["q"] == "P" or qs[d] is None else 1) for d in nd["deps"]] for nd in nodes]
    succ = [[] for nd in nodes]
    for i in range(n):
        for d, w in pred[i]:
            succ[d].append((i, w))
    banks = [([r[0] for it in nd["items"] for r in it["reads"] + it["writes"] if r[0] not in SB] + [None])[0] for nd in nodes]
    cases = []
    for f, gat, sca, fix, wake, far in OPT["cases"]:
        cases.append(([f * (nd["dur"][0] + gat * nd["dur"][1] + sca * nd["dur"][2]) + fix * nd["dur"][3] for nd in nodes],
                      [nd["lat"] * (far if nd["far"] else 1.0) for nd in nodes], wake))

    def play(seq, case):
        dur, lat, wake = case
        end, free, used = [0.0] * n, {}, {}
        for i in seq:
            t = free.get(qs[i], 0.0)
            for d, w in pred[i]:
                if end[d] + w * wake > t:
                    t = end[d] + w * wake
            b = banks[i]
            if b:
                u = used.setdefault(b, {})
                for q in u:
                    if q != qs[i] and u[q] + wake > t:
                        t = u[q] + wake
                u[qs[i]] = t + dur[i]
            if qs[i]:
                free[qs[i]] = t + dur[i]
            end[i] = t + dur[i] + lat[i]
        return max(end)

    def deal(way, back, case, tol):
        dur, lat, wake = case
        before, after = (succ, pred) if back else (pred, succ)
        left = [len(p) for p in before]
        ready, end, seq = [0.0] * n, [0.0] * n, []
        pool, free, used = {q: [] for q in (None, "V", "S", "P", "G", "Y")}, {q: 0.0 for q in "VSPGY"}, {}
        for i in range(n):
            if not left[i]:
                ready[i] = lat[i] if back else 0.0
                pool[qs[i]].append(i)
        while len(seq) < n:
            if pool[None]:
                i = pool[None].pop()
                t = ready[i]
            else:
                now, q, at = 1e18, None, None
                for q2 in "VSPGY":
                    if pool[q2] and free[q2] < now:
                        a2 = []
                        for j in pool[q2]:
                            t = ready[j] if ready[j] > free[q2] else free[q2]
                            if banks[j] in used:
                                for q3, e in used[banks[j]].items():
                                    if q3 != q2 and e + wake > t:
                                        t = e + wake
                            a2.append((t, j))
                        t2 = min(a2)[0]
                        if t2 < now:
                            now, q, at = t2, q2, a2
                near = [(way[j], t, j) for t, j in at if t <= now + tol[0]]
                w, t, i = max(near)
                if t > now:
                    fits = [e for e in near if e[1] < t and e[1] + dur[e[2]] <= t + tol[1] + tol[2] * (t - e[1])]
                    if fits:
                        w, t, i = max(fits)
                pool[q].remove(i)
                free[q] = t + dur[i]
                if banks[i]:
                    used.setdefault(banks[i], {})[q] = t + dur[i]
            end[i] = t + dur[i] + (0.0 if back else lat[i])
            seq.append(i)
            for j, w in after[i]:
                ready[j] = max(ready[j], end[i] + w * wake + (lat[j] if back else 0.0))
                left[j] -= 1
                if not left[j]:
                    pool[qs[j]].append(j)
        return seq, end

    def score(seq):
        return sum(play(seq, c) / s for c, s in zip(cases, OPT["scale"]))

    kinds = {}
    for i in range(n):
        w = nodes[i]["items"][0]["writes"] if nodes[i]["items"] else []
        kinds.setdefault((qs[i], w[0][0] if w else "", nodes[i]["step"]), []).append(i)
    kinds = list(kinds.values())
    dur, lat, wake = cases[0]
    way = [0.0] * n
    for i in range(n - 1, -1, -1):
        way[i] = dur[i] + lat[i] + max([way[j] + w * wake for j, w in succ[i]] + [0.0])
    tol = list(OPT["tol"])
    seq, end = deal(way, False, cases[0], tol)
    best = top = (score(seq), seq, way, end, tol)
    for it in range(OPT["moves"]):
        way, tol = list(best[2]), list(best[4])
        r = rnd()
        if r < OPT["turn"]:
            way = deal(best[3], True, cases[0], tol)[1]
        elif r < OPT["turn"] + 0.05:
            tol = [a * (0.6 + 0.8 * rnd()) for a in OPT["tol"]]
        else:
            for _ in range(1 + int(3 * rnd())):
                by = (rnd() - 0.5) * 5000.0 * rnd()
                for i in kinds[int(rnd() * len(kinds))]:
                    way[i] += by
        seq, end = deal(way, False, cases[0], tol)
        now = (score(seq), seq, way, end, tol)
        if now[0] <= best[0] * (1 + OPT["slack"] * (1 - it / OPT["moves"]) * rnd()):
            best = now
            if now[0] < top[0]:
                top = now
    PLAN["times"] = [round(play(top[1], c)) for c in cases]
    return top[1]


def rank_program(g, core, T, topo):
    rank = T.rank_of(core)
    if rank is None:
        return
    N = len(T.cores)
    Op, Fn = AluOpType, ActivationFunctionType
    QU = {"V": g.vector, "S": g.scalar, "P": g.tensor, "G": g, "Y": g.sync}
    size = {k: n for k, (n, d) in SB.items()}
    size.update({"ps%d" % b: 512 for b in range(8)})
    nodes, macro, group, opened, ndma, step = [], [], {}, {}, [0], [-1]
    nwr = {k: np.full(n, -1) for k, n in size.items()}
    nrd = {k: [] for k in size}

    def A(name, a=0, b=None, s=1, p=None):
        if b is None:
            b = size[name]
        ps = slice(0, 128) if p is None else p
        buf, o = PLACE.get(name, (name, 0))
        two = name in SB and BYTES[SB[name][1]] == 2
        return {"ap": T[buf][ps, o + a:o + b:s] if s != 1 else T[buf][ps, o + a:o + b], "r": [(name, slice(a, b, s))],
                "n": len(range(a, b, s)), "two": two, "ps": name not in SB}

    def IND(win, off):
        return {"ap": win["ap"].indirect(off["ap"]), "r": win["r"], "x": off["r"], "n": 16 * off["n"], "two": False, "ps": False}

    def wide(reg):
        name, sl = reg
        e = 16 // BYTES[SB[name][1]]
        return name, slice(sl.start // e * e, min(-(-sl.stop // e) * e, size[name]), 1)

    def node(q, items, dur, lat=0.0, acc=None, after=()):
        reads = [r for it in items for r in it["reads"]]
        writes = [r for it in items for r in it["writes"]]
        me, deps = len(nodes), set(after)
        if q == "P":
            st = opened.setdefault(writes[0][0], {"stop": -1, "whole": []})
            if acc in (None, "start"):
                deps.add(st["stop"])
            if acc is None:
                st["whole"].append(me)
            elif acc == "start":
                deps.update(st["whole"])
                st["whole"] = []
            elif acc == "stop":
                st["stop"] = me
        if acc in ("mid", "stop"):
            name = writes[0][0]
            deps.update(group[name]["ops"] if acc == "stop" else group[name]["ops"][:1])
            group[name]["ops"].append(me)
            writes = group[name]["regs"] if acc == "stop" else []
        for name, sl in reads + writes:
            deps.update(int(o) for o in np.unique(nwr[name][sl]))
        for name, sl in writes:
            mark = np.zeros(size[name], bool)
            mark[sl] = True
            deps.update(o for o, s2 in nrd[name] if mark[s2].any())
        if acc == "start":
            group[writes[0][0]] = {"ops": [me], "regs": list(writes)}
        for name, sl in reads:
            nrd[name].append((me, sl))
        for name, sl in writes:
            nwr[name][sl] = me
            mark = np.zeros(size[name], bool)
            mark[sl] = True
            nrd[name] = [(o, s2) for o, s2 in nrd[name] if o == me or not mark[s2].all()]
        deps.discard(-1)
        deps.discard(me)
        nodes.append({"q": q, "items": items, "dur": dur, "lat": lat, "deps": sorted(deps), "step": step[0], "far": False})
        return me

    def call(q, fn, out, ins, per=None, acc=None):
        reads, writes = list(out.get("x", [])), list(out["r"])
        ins = [x for x in ins if isinstance(x, dict)]
        for x in ins:
            reads += x["r"] + x.get("x", [])
        n = max(out["n"], ins[0]["n"] if ins else 0)
        if q == "P":
            dur = [max(64, out["n"]) * CYC / 2 * (1.0 if ins[0]["two"] else 4.0), 0, 0, 0]
        elif q == "G":
            dur = [140.0 + 2 * n * CYC, 0, 0, 0]
        elif "x" in out:
            dur = [50.0, 0, out["n"] * CYC, 0]
        elif ins and "x" in ins[0]:
            dur = [50.0 if q == "V" else 65.0, out["n"] * CYC, 0, 0]
        elif q == "S":
            dur = [65.0 + n * CYC, 0, 0, 0]
        else:
            dur = [CYC * max(64.0, n * (per or (0.5 if all(x["two"] or x["n"] == 1 for x in [out] + ins) else 1.0))), 0, 0, 1]
        it = {"kind": "c", "q": q, "fn": fn, "reads": reads, "writes": writes}
        if macro:
            macro[0].append(it)
            macro[1] = [a + b for a, b in zip(macro[1], dur)]
        else:
            node(q, [it], dur, acc=acc)

    def together(q, body, acc=None):
        macro.extend([[], [0, 0, 0, 0]])
        body()
        items, dur = macro
        del macro[:]
        node(q, items, dur, acc=acc)

    def emit(seq):
        cnt = {"V": 0, "S": 0, "P": 0, "G": 0}
        known = {q: {} for q in QU}
        done, tails = [], {}
        wr = {k: np.full(n, -1) for k, (n, d) in SB.items()}
        rd = {k: {} for k in SB}
        bank = {"ps%d" % b: {} for b in range(8)}

        def order(q, eng, reads, writes):
            deps = set()
            for name, sl in reads + writes:
                if name in bank:
                    deps.update(o for e, o in bank[name].items() if e != eng)
                else:
                    deps.update(int(o) for o in np.unique(wr[name][sl]))
            for name, sl in writes:
                if name not in bank:
                    for arr in rd[name].values():
                        deps.update(int(o) for o in np.unique(arr[sl]))
            deps.discard(-1)
            for o in sorted(deps, reverse=True):
                sem, c, clock = done[o]
                if known[q].get(sem, 0) < c:
                    QU[q].wait_ge(T.sem[sem], c)
                    for k2, c2 in clock.items():
                        if known[q].get(k2, 0) < c2:
                            known[q][k2] = c2

        def note(q, eng, sem, c, reads, writes):
            clock = dict(known[q]) if q else {}
            clock[sem] = c
            done.append((sem, c, clock))
            o = len(done) - 1
            tails[sem] = c
            for name, sl in reads + writes:
                if name in bank:
                    bank[name][eng] = o
            for name, sl in reads:
                if name not in bank:
                    if eng not in rd[name]:
                        rd[name][eng] = np.full(size[name], -1)
                    rd[name][eng][sl] = o
            for name, sl in writes:
                if name not in bank:
                    wr[name][sl] = o
                    for arr in rd[name].values():
                        arr[sl] = -1

        for i in seq:
            for it in nodes[i]["items"]:
                q = it["q"]
                if it["kind"] == "c":
                    order(q, q, it["reads"], it["writes"])
                    cnt[q] += 1
                    it["fn"]().then_inc(T.sem["s" + q], 1)
                    note(q, q, "s" + q, cnt[q], it["reads"], it["writes"])
                elif it["kind"] == "in":
                    note(None, it["sem"], it["sem"], it["c"], [], it["writes"])
                else:
                    order(q, it["sem"], it["reads"], it["writes"])
                    it["fn"]()
                    note(q, it["sem"], it["sem"], it["c"], it["reads"], it["writes"])
        for sem, c in tails.items():
            if known["G"].get(sem, 0) < c:
                g.wait_ge(T.sem[sem], c)

    def ap(x):
        return x["ap"] if isinstance(x, dict) else x

    def cp(out, in_):
        call("V", lambda: g.vector.tensor_copy(out["ap"], in_["ap"]), out, [in_])

    def tt(out, a, b, op):
        call("V", lambda: g.vector.tensor_tensor(out["ap"], a["ap"], b["ap"], op), out, [a, b], per=1.0 if a["ps"] or b["ps"] else 2.0)

    def ts(out, a, s1, o1, s2=None, o2=None):
        if o2 is None:
            call("V", lambda: g.vector.tensor_scalar(out["ap"], a["ap"], ap(s1), None, o1), out, [a, s1])
        else:
            call("V", lambda: g.vector.tensor_scalar(out["ap"], a["ap"], ap(s1), ap(s2), o1, o2), out, [a, s1, s2])

    def scan(out, d0, d1, init, o0, o1):
        call("V", lambda: g.vector.tensor_tensor_scan(out["ap"], d0["ap"], d1["ap"], init, o0, o1), out, [d0, d1])

    def red(out, in_, op):
        call("V", lambda: g.vector.tensor_reduce(out["ap"], in_["ap"], AxisListType.X, op), out, [in_])

    def tr(out, in_):
        call("V", lambda: g.vector.transpose(out["ap"], in_["ap"]), out, [in_])

    def mset(out, c):
        call("V", lambda: g.vector.memset(out["ap"], c), out, [])

    def act(out, in_, fn, bias=0.0, scale=1.0):
        call("S", lambda: g.scalar.activation(out["ap"], in_["ap"], fn, bias=ap(bias), scale=ap(scale)), out, [in_, bias, scale])

    def gather(on, out, win, off):
        x = IND(win, off)
        if on == "S":
            call("S", lambda: g.scalar.activation(out["ap"], x["ap"], Fn.Copy), out, [x])
        else:
            cp(out, x)

    def mm(out, lhsT, rhs, start, stop):
        call("P", lambda: g.tensor.matmul(out["ap"], lhsT["ap"], rhs["ap"], start, stop), out, [lhsT, rhs],
             acc=None if start and stop else "start" if start else "stop" if stop else "mid")

    def iota(out, pat, base, cm):
        if SB[out["r"][0][0]][1] == i32:
            call("G", lambda: g.iota(out["ap"], pat, base, cm), out, [])
        else:
            call("G", lambda: g.iota(out["ap"], pat, base, cm, allow_small_or_imprecise_dtypes=True), out, [])

    def fill(out, c):
        iota(out, [[0, out["n"]]], c, 0)

    def lower(out, in_):
        call("G", lambda: g.affine_select(out["ap"], in_["ap"], [[1, 128]], Op.is_gt, 0.0, 0, -1), out, [in_])

    def dma(q, out, in_, lat=2500.0):
        sem = "d%d" % ndma[0]
        ndma[0] += 1
        reads = [wide(r) for r in in_["r"]] if isinstance(in_, dict) else []
        writes = [wide(r) for r in out["r"]] if isinstance(out, dict) else []
        node(q, [{"kind": "d", "q": q, "sem": sem, "c": 16, "reads": reads, "writes": writes,
                  "fn": lambda: QU[q].dma_start(ap(out), ap(in_)).then_inc(T.sem[sem], 16)}], [60.0, 0, 0, 0], lat)

    def remote(fn, src, lsem, nl, dst, rsem, nr, lat):
        me = node("G", [{"kind": "r", "q": "G", "sem": lsem, "c": nl, "reads": [wide(r) for r in src["r"]], "writes": [], "fn": fn}],
                  [900.0, 0, 0, 0], lat + (0.0 if any(nd["far"] for nd in nodes) else OPT["first"]))
        nodes[me]["far"] = True
        node(None, [{"kind": "in", "q": None, "sem": rsem, "c": nr, "reads": [], "writes": dst["r"]}], [1.0, 0, 0, 0], 200.0, after=[me])

    def bits(m):
        return bin(m).count("1")

    def send(src, dstbuf, shift, rsem, lsem):
        to, fr = T.cores[(rank + shift) % N], T.cores[(rank - shift) % N]
        rid, pid, _ = topo.addr(to)
        m = topo.mask(core, to)
        remote(lambda: g.remote_dma(dstbuf["ap"], src["ap"], T.sem[rsem], T.sem[lsem], pid, rid, m),
               src, lsem, bits(m), dstbuf, rsem, bits(topo.mask(fr, core)), OPT["far"])

    def fan_plan(c):
        far = [x for x in T.cores if topo.chip(x) != topo.chip(c)]
        near = [x for x in T.cores if topo.chip(x) == topo.chip(c) and x != c]
        mf = -1
        for x in far:
            mf &= topo.mask(c, x)
        plan = [(far, mf)]
        if near:
            es = [e for e in topo.engines(c, near[0]) if not mf >> e & 1][:2]
            plan.append((near, sum(1 << e for e in es)))
        return plan

    def send_all(name, w, rsem, lsem):
        src, trs, tot = A(name, 4 - w, 4), [], 0
        for dsts, m in fan_plan(core):
            js = [(T.rank_of(x) - rank - 1) % N for x in dsts]
            trs.append(RemoteDMATransfer(dst_ids=[DstId(rid=topo.addr(x)[0], pnc=topo.addr(x)[1]) for x in dsts],
                                         dma_engine_mask=m, remote_sem=T.sem[rsem], src=src["ap"],
                                         dsts=[A(name, 4 + w * j, 4 + w * j + w)["ap"] for j in js]))
            tot += bits(m)
        got = sum(bits(m) for x in T.cores if x != core for dsts, m in fan_plan(x) if core in dsts)
        remote(lambda: g.remote_dma_fused(trs, local_sem=T.sem[lsem]), src, lsem, tot, A(name, 4, 4 + w * (N - 1)), rsem, got, OPT["fan"])

    def PS(b, a, e, s=1):
        return A("ps%d" % b, a, e, s)

    def sel(name, r):
        return A(name, 15 - r, 143 - r)

    def pc(j):
        return A("pc", j, j + 1)

    def to_list(out, name, src, a):
        together("P", lambda: [mm(out, sel(name, r), A(src, a + r, a + L, 16), r == 0, r == 15) for r in range(16)])

    def swap(b, a, src, stride, parts):
        ways = [(kind, e, gg) for kind, e in parts for gg in range(2)]
        together("P", lambda: [mm(PS(b, a + h, a + 10, 2), A("%s%d%d" % (kind, h, gg)), A(src, stride * gg + e, 10 * stride, 2 * stride),
                                  j == 0, j == len(ways) - 1) for h in range(2) for j, (kind, e, gg) in enumerate(ways)])

    col = A("colx", C0, C0 + W)
    BIG = 8179.75
    HALF = BIG + 0.5 - 1.0 / 32
    TH0 = BIG + 2.0 - 1.0 / 32
    R16, R1 = 1.5 * 2 ** 19, 1.5 * 2 ** 23

    dma("S", A("odl"), T.od[:])
    dma("Y", col, T.nb[:], 7500.0)
    dma("Y", A("X"), T.xs[:], 10000.0)
    nodes[-2]["items"] += nodes[-1]["items"]
    nodes[-1].update({"q": None, "items": [], "dur": [0, 0, 0, 0], "lat": 2700.0, "deps": [len(nodes) - 2]})
    dma("S", A("thl", p=slice(0, 8)), T.th[:])
    dma("S", A("wtl"), T.wt[:])

    iota(A("pI"), [[0, 1]], 0, 1)
    iota(A("pf"), [[0, 1]], 0, 1)
    iota(A("xm16"), [[0, 8], [1, 16]], 0, 0)
    iota(A("g16"), [[16, 8], [0, 16]], 0, 0)
    iota(A("Dg"), [[1, 128]], 0, -1)
    iota(A("xs1"), [[1, 144]], -15, 0)
    iota(A("g32"), [[32, 4], [0, 32]], 0, 0)
    iota(A("ln"), [[32, 5], [0, 2]], 0, 1)
    iota(A("qq"), [[16, 10]], L, 1)
    iota(A("gg"), [[0, 15], [1, 2]], 0, 0)
    iota(A("PL"), [[1, 128]], 0, 0)
    for name, a, b, c in (("colx", 0, C0, 0), ("colx", C0 + W, SD, 0), ("VW0", L, NX, 0), ("VW1", L, NX, 0), ("ones", 0, L, 1),
                          ("patA", 0, L, 0), ("fI", 0, 60, 0), ("d5", 0, 60, 0), ("CT", 0, 60, 1), ("fr", 0, 10, 32768),
                          ("mOld", 0, 10, 32768), ("JT", 0, 32, 0), ("mZ", 0, L, 0), ("gZ", 0, L, 0), ("mw", 0, 2 * L, 0)):
        fill(A(name, a, b), c)
    mset(A("patA", 15, L, 16), BIG)
    mset(A("d5", 5, 60, 6), 1.0)
    for ch, c in ((0, -416.5 * 32768), (1, NX / 1024), (2, (NX + U) / 1024), (4, 352.0 / 1024)):
        mset(A("CT", ch, 60, 6), c)
    for j, m in enumerate((112, 96, 15, 16)):
        ts(A("pJ", j, j + 1), A("pI"), m, Op.bitwise_and)
    cp(A("pc", 0, 4), A("pJ"))
    ts(A("mask"), A("xm16", 0, 16), pc(2), Op.is_equal)
    ts(pc(4), pc(2), -128.0, Op.mult)
    ts(A("BOh"), A("g16"), pc(0), Op.is_equal)
    cp(A("od16"), A("odl"))
    for r in range(16):
        ts(A("odD", r, Q, 16), A("odl"), A("mask", r, r + 1), Op.mult)
    for j in range(2):
        mm(PS(6 + j, 0, 480), A("BOh"), A("odD", 480 * j, 480 * j + 480), True, True)
        act(A("ptmp"), PS(6 + j, 0, 480), Fn.Relu, bias=pc(4))
        act(A("P1", 480 * j, 480 * j + 480), A("ptmp"), Fn.Relu, bias=128.0, scale=-1.0)
    act(A("VW0", 0, L), A("P1", 0, L), Fn.Copy)
    act(A("VW0", NX, NX + L), A("P1", L, 2 * L), Fn.Copy)
    ts(A("sd16"), A("odl", 0, 10), C0 - 1.0, Op.add)
    ts(A("If"), A("Dg"), 0.0, Op.is_equal)
    for name, c in (("Ib", 1.0), ("In", -1.0), ("Ih", 1.0), ("Iy", 1.0 / 512), ("IB", 32768.0)):
        ts(A(name), A("Dg"), 0.0, Op.is_equal, c, Op.mult)
    cp(A("oneH"), A("ones"))
    ts(A("BO"), A("g16"), pc(0), Op.is_equal)
    ts(A("BON16"), A("g16"), pc(0), Op.is_equal, -1.0, Op.mult)
    for kv in sorted(set(OPT["kv"][2:] + OPT["ko"]) - {16}):
        ts(A("tn"), A("xm16", 0, 128), float(kv), Op.is_lt)
        tt(A("BON%d" % kv), A("tn"), A("BON16"), Op.mult)
    ts(A("SEL2"), A("xs1"), pc(0), Op.is_equal, 2.0, Op.mult)
    ts(A("SELN"), A("xs1"), pc(0), Op.is_equal, -1.0, Op.mult)
    ts(A("SEL1"), A("xs1"), pc(0), Op.is_equal)
    ts(pc(5), pc(2), 1.0 / 16, Op.mult, -415.0 / 1024, Op.add)
    ts(pc(6), pc(2), 15.0, Op.is_equal, 8192.0, Op.mult)
    ts(pc(10), pc(2), 0.0, Op.is_gt, -1.0, Op.mult)
    ts(pc(7), pc(10), -4096.0, Op.mult, 4096.0, Op.add)
    for h in range(2):
        ts(pc(8 + h), pc(3), 16.0 * h, Op.is_equal, 1024.0, Op.mult)
        ts(pc(12 + h), pc(3), 16.0 * h, Op.is_equal, 32768.0, Op.mult)
        ts(A("tn"), A("g16"), pc(1), Op.subtract, 16.0 * h, Op.is_equal)
        ts(A("NF%d" % h), A("tn"), 1.0 / 32768, Op.mult)
    ts(A("KC"), A("Ib"), pc(5), Op.mult)
    ts(A("DC"), A("Ib"), pc(6), Op.mult)
    ts(A("tm"), A("Dg"), -1.0, Op.is_equal, pc(10), Op.mult)
    tt(A("tm"), A("tm"), A("Ib"), Op.add)
    ts(A("DM"), A("tm"), 1.0 / 1024, Op.mult)
    ts(A("DY"), A("tm"), -66.0 / 1024, Op.mult)
    ts(A("O32f"), A("g32"), pc(1), Op.is_equal)
    ts(A("O32"), A("g32"), pc(1), Op.is_equal, 1.0 / 1024, Op.mult)
    ts(A("OG"), A("g32"), pc(1), Op.is_equal, -32768.0, Op.mult)
    lower(A("L32"), A("O32"))
    lower(A("tl"), A("OG"))
    ts(A("tk"), A("Dg"), 0.0, Op.is_equal, 512.0 * 32768, Op.mult)
    tt(A("LG"), A("tl"), A("tk"), Op.add)
    ts(A("d5", 2, 60, 6), A("ln"), pc(1), Op.subtract, 1.0 / 1024, Op.mult)
    ts(A("lanec"), A("ln"), pc(1), Op.subtract, 672.0, Op.add)
    for h in range(2):
        for gg in range(2):
            ts(A("PH%d%d" % (h, gg)), A("Dg"), 16.0 * (gg - h), Op.is_equal, pc(8 + h), Op.mult)
            ts(A("PB%d%d" % (h, gg)), A("Dg"), 16.0 * (gg - h), Op.is_equal, pc(12 + h), Op.mult)
    ts(A("nx0"), A("qq"), pc(0), Op.subtract)
    cp(A("wf"), A("wtl"))
    ts(A("SELW"), A("SEL1"), A("wf"), Op.mult)
    p8 = slice(0, 8)
    ts(A("pK", p=p8), A("pI", p=p8), 6, Op.bitwise_and)
    cp(A("thf", p=p8), A("thl", p=p8))
    ts(A("pd", 0, 1, p=p8), A("pK", p=p8), 15.0, Op.mult, A("pf", p=p8), Op.add)
    ts(A("PL", p=p8), A("PL", p=p8), A("pd", 0, 1, p=p8), Op.is_equal)
    ts(A("ggm"), A("gg"), pc(1), Op.add, A("pf"), Op.is_equal)
    mm(PS(2, 200, 201), A("PL", p=p8), A("thf", p=p8), True, True)
    ts(A("thK", 0, 1), PS(2, 200, 201), TH0, Op.add)
    ts(A("thK", 1, 2), PS(2, 200, 201), TH0, Op.add)

    def limits(t):
        if t == 0 or t >= 3:
            act(A("thr"), A("ggm"), Fn.Identity, bias=-1.0 / 16, scale=A("thK", max(t - 1, 0), max(t - 1, 0) + 1))
        more = [(442, "IB", A("un")), (452, "IB", A("un")), (462, "IB", A("un"))] if t >= 3 else []
        if t >= 3:
            mm(PS(5, 432, 442), A("O32f"), A("thr", 0, 10), True, True)
            tt(A("un"), A("mOld"), PS(5, 432, 442), Op.is_lt)
        more += [(452, "Ib", A("fr")), (462, "In", A("fr")), (462, "IB", A("ones", 0, 10))]
        together("P", lambda: [mm(PS(5, 442, 472), A("O32f"), A("thr"), True, False)]
                 + [mm(PS(5, a, a + 10), A(w), x, False, j == len(more) - 1) for j, (a, w, x) in enumerate(more)])

    def distances(lo, hi, last, rec, a, mx, key, copy, b, kv):
        n = hi - lo
        per = 512 // n
        for k0 in range(kv, 16, per):
            k1 = min(16, k0 + per)
            for k in range(k0, k1):
                o = PS(b, n * (k - k0), n * (k - k0) + n)
                together("P", lambda: [mm(o, A("In"), A(rec, lo, hi), True, False), mm(o, A("Ib"), A(a, 16 * lo + k, 16 * hi, 16), False, True)])
            act(A(mx, 16 * lo + n * k0, 16 * lo + n * k1), PS(b, 0, n * (k1 - k0)), Fn.Abs)
            for k in range(k0, k1):
                mm(PS(key, lo, hi), sel("SEL1", k), A(mx, 16 * lo + n * k, 16 * lo + n * k + n), False, last and kv == 0 and k == 15)
        for k0 in range(0, kv, 4):
            together("P", lambda: [mm(PS(key, lo, hi), sel("SELN", k), A(a, 16 * lo + k, 16 * hi, 16), False, False)
                                   for k in range(k0, min(kv, k0 + 4))], "mid")
        for k in range(kv):
            m = A(mx, 16 * lo + n * k, 16 * lo + n * k + n)
            tt(m, A(a, 16 * lo + k, 16 * hi, 16), PS(0, copy + lo, copy + hi), Op.max)
            mm(PS(key, lo, hi), sel("SEL2", k), m, False, last and k == kv - 1)

    def hop(t):
        return 1 + (t - 1) % (N - 1)

    def places(t):
        to_list(PS(2, 224, 234), "SELW", "gx%d" % t, 0)
        ts(A("hi"), PS(2, 224, 234), 77.0 * t, Op.add)
        ts(A("hj"), A("hi"), W - 1, Op.bitwise_and)
        cp(A("h%d" % t), A("hj"))

    def guests(t):
        gx, kv, gc, ga = "gx%d" % t, OPT["kv"][t], "gc%d" % (t % 2), "ga%d" % (t % 2)
        cp(A(gc), IND(col, A("h%d" % t)))
        for lo, hi, on in OPT["gcuts"][t]:
            gather(on, A(ga, 16 * lo, 16 * hi), A("X"), A(gc, lo, hi))
        mm(PS(4, 0, L), A("BON%d" % kv), A(gx), True, False)
        mm(PS(0, 256, 256 + L), A("Ib"), A(gx), True, True)
        ch = OPT["gchunks"][t]
        for j in range(len(ch) - 1):
            distances(ch[j], ch[j + 1], j == len(ch) - 2, gx, ga, "gab", 4, 256, 6, kv)
        tr(A("gT"), PS(4, 0, L))
        scan(A("GS%d" % (t % 2)), A("gT"), A("patA"), 2 * BIG, Op.min, Op.add)
        if t in OPT["back"]:
            cp(A("dm%d" % t, 0, 10), A("GS%d" % (t % 2), 15, L, 16))
            send(A("dm%d" % t, 0, 10), A("gm%d" % t, 0, 10), -hop(t), "am%d" % t, "lm%d" % t)

    def judge(t):
        fan = [f for f in OPT["fans"] if t in f][0]
        mine = A("lv%d" % t, 0, 10) if t in OPT["back"] else A("GS%d" % (t % 2), 15, L, 16)
        tt(A("gJ"), mine, A("gm%d" % t, 0, 10), Op.min)
        for gg in range(2):
            red(A("JT", gg, gg + 1), A("gJ", gg, 10, 2), Op.max)
        tr(A("JU"), A("JT"))
        e = 4 - len(fan) + fan.index(t)
        red(A("rb%d" % fan[-1], e, e + 1), A("JU"), Op.max)
        if t == fan[-1]:
            send_all("rb%d" % t, len(fan), "ab%d" % t, "lb%d" % t)

    def raise_limits(t):
        fan = [f for f in OPT["fans"] if t in f][0]
        w = len(fan)
        red(A("br"), A("rb%d" % fan[-1], 4 - w + fan.index(t), 4 + w * (N - 1), w), Op.max)
        ts(A("b2"), A("br"), A("thK", t - 1, t), Op.subtract, 0.25, Op.mult)
        name = "thK"
        if t == NT - 1:
            name = "tho"
            ts(A("tho", 0, t), A("thK", 0, t), -TH0, Op.add)
        ts(A(name, t, t + 1), A("b2"), 0.0, Op.max, A(name, t - 1, t), Op.add)

    def guest_rows(t):
        ts(A("gZ", 15, L, 16), A("gJ"), -HALF, Op.add, R1, Op.add)
        tr(A("gY"), A("gZ"))
        ts(IND(A("mw"), A("sl16")), A("gY"), 1.0, Op.mult, -R1, Op.add)
        send(A("mw", 0, U), A("gw"), hop(t), "ag", "lg")
        dma("S", T.yg[:], A("gw", p=slice(15, 128, 16)))

    def leavers(t):
        tt(A("lv%d" % (t + 1), 0, 10), A("mS"), PS(3, 0, 60, 6), Op.min)
        if t + 1 not in OPT["back"]:
            send(A("lv%d" % (t + 1), 0, 10), A("gm%d" % (t + 1), 0, 10), hop(t + 1), "am%d" % (t + 1), "lm%d" % (t + 1))
        if t == NT - 2:
            ts(A("st1"), PS(3, 0, 60, 6), -1.0 / 32768, Op.mult, 95.5, Op.add)
            tt(A("st2"), A("lanec"), A("st1"), Op.subtract)
            tt(A("slT"), A("st1"), A("st2"), Op.min)
            swap(2, 32, "slT", 1, [("PH", 0)])
            ts(A("sl16"), PS(2, 32, 42), 1.0 / 1024, Op.mult)

    def seeds():
        cp(A("colx", C0 - 1, C0), A("colx", C0 + W - 1, C0 + W))
        ts(A("stmp"), IND(A("colx", 0, C0 + W), A("sd16")), 1.0, Op.add)
        ts(A("colx", SD, SD + L), A("stmp"), W - 1, Op.bitwise_and)

    for t in range(NT):
        last = t == NT - 1
        step[0] = t
        own, vw = A("own%d" % (t % 2)), "VW%d" % (t % 2)
        if t == 0:
            seeds()
            cp(A("c16"), A("colx", SD, SD + L))
            v16 = A("od16", 0, 10)
        else:
            ts(A("off1"), PS(5, 0, 10), C0 - 9409.0, Op.add)
            cp(A("c16"), IND(A("colx"), A("off1")))
            cp(A("off2"), PS(2, 0, 10))
            gather("S", A(vw, 0, L), A("VW%d" % ((t - 1) % 2)), A("off2"))
            to_list(PS(2, 176, 186), "SELN", vw, 0)
            v16 = A("v16")
            ts(v16, PS(2, 176, 186), 2048.0, Op.add)
        gather("S", own, A("X"), v16)
        for lo, hi, on in OPT["cuts"][t]:
            gather(on, A("a", 16 * lo, 16 * hi), A("X"), A("c16", lo, hi))
        if t < NT - 2:
            send(own, A("gx%d" % (t + 2)), hop(t + 2), "ax%d" % (t + 2), "lx%d" % (t + 2))
        cp(A("cH"), A("c16"))
        ts(A("yy"), A("c16"), 1.0 / 64, Op.mult, 192.0 - 31.5 / 64, Op.add)
        mm(PS(0, 0, L), A("Ib"), own, True, True)
        mm(PS(1, 0, L), A("KC"), A("oneH"), True, False)
        mm(PS(1, 0, L), A("BON%d" % OPT["ko"][t]), own, False, False)
        mm(PS(1, 0, L), A("Iy"), A("yy"), False, False)
        together("P", lambda: [mm(PS(5, 64, 64 + L), A("BO"), A(vw, 0, L), True, False), mm(PS(5, 64, 64 + L), A("Ih"), A("cH"), False, True)])
        act(A("ad"), PS(5, 64, 64 + L), Fn.Abs, bias=-2048.0)
        ts(A("pen"), A("ad"), 16.0, Op.is_lt, pc(7), Op.mult)
        mm(PS(1, 0, L), A("Ib"), A("pen"), False, False)
        cp(IND(col, v16), A("c16"))
        if t >= 2:
            judge(t)
        if 1 <= t < NT - 1:
            guests(t + 1)
        if t < NT - 2:
            places(t + 2)
        if last:
            guest_rows(t)
            mm(PS(5, 256, 256 + L), A("BO"), A(vw, 0, L), True, True)
            act(A("ov"), PS(5, 256, 256 + L), Fn.Identity, bias=2048.0, scale=-1.0)
            dma("Y", T.yv[:], A("ov", p=slice(0, 128, 16)))
            for a, b in zip(OPT["out"], OPT["out"][1:]):
                cp(A("on", 16 * a, 16 * b), IND(col, A("od16", a, b)))
                dma("Y", T.yn[:, 16 * a:16 * b], A("on", 16 * a, 16 * b), 2200.0 + 40.0 * b)
        else:
            if t >= 1:
                together("P", lambda: [mm(PS(2, 192, 193), A("NF%d" % (j % 2)), A("fr", j, j + 1), j == 0, j == 9) for j in range(10)])
                ts(A("nx%d" % (t % 2)), A("nx%d" % ((t - 1) % 2)), PS(2, 192, 193), Op.add)
                gather("S", A(vw, NX, NX + L), A("P1", 0, L * (t + 2)), A("nx%d" % (t % 2)))
            together("P", lambda: [mm(PS(3, 0, L), A("DC"), A("oneH"), True, False), mm(PS(3, 0, L), A("DY"), A("yy"), False, False),
                                   mm(PS(3, 0, L), A("DM"), A("cH"), False, True)])
            tr(A("TD"), PS(3, 0, L))
            mm(PS(3, 0, 60), A("If"), A("CT"), True, False)
            to_list(PS(2, 240, 250), "SELN", vw, NX)
            ts(A("sd16"), PS(2, 240, 250), 2048.0 + C0 - 1, Op.add)
            seeds()
            if t >= 3:
                raise_limits(t - 1)
            limits(t)
        ch = OPT["chunks"][t]
        for j in range(len(ch) - 1):
            distances(ch[j], ch[j + 1], j == len(ch) - 2, own["r"][0][0], "a", "mx", 1, 0, 7, OPT["ko"][t])
        tr(A("TK"), PS(1, 0, L))
        scan(A("S", 0, L), A("TK"), A("patA"), 2 * BIG, Op.min, Op.add)
        SA = A("S", 15, L, 16)
        if last:
            tt(A("mS"), SA, A("mOld"), Op.min)
            ts(A("oi"), A("mS"), -HALF, Op.add, 4095.0, Op.min)
            cp(A("mZ", 15, L, 16), A("oi"))
            tr(A("mT"), A("mZ"))
            dma("S", T.ym[:], A("mT", p=slice(15, 128, 16)))
            raise_limits(t - 1)
            raise_limits(t)
            for gg in range(2):
                dma("YS"[gg], T.yt[gg:8:2, :], A("tho", 0, NT, p=slice(gg, 128, 32)))
            break
        tt(A("go"), SA, PS(5, 452, 462), Op.is_ge)
        tt(A("fI", 1, 60, 6), SA, PS(5, 462, 472), Op.is_lt)
        tt(A("fI", 2, 60, 6), SA, PS(5, 442, 452), Op.is_lt)
        tt(A("d5", 0, 60, 6), SA, PS(5, 442, 452), Op.is_lt)
        mm(PS(3, 0, 60, 6), A("LG"), A("go"), False, False)
        for s in range(1, 5):
            mm(PS(3, 12 * s, 60, 6), A("OG"), A("go", 0, 10 - 2 * s), False, False)
        mm(PS(3, 0, 60), A("L32"), A("fI"), False, False)
        for s in range(1, 5):
            mm(PS(3, 12 * s, 60), A("O32"), A("fI", 0, 60 - 12 * s), False, s == 4)
        scan(A("S", L, 2 * L), A("TK"), A("TD"), 2 * BIG, Op.min, Op.add)
        ts(A("Fk"), SA, R16, Op.add, -R16 - 320.0 / 1024, Op.add)
        tt(A("d5", 4, 60, 6), SA, A("Fk"), Op.subtract)
        tt(A("d5", 3, 60, 6), A("S", L + 15, 2 * L, 16), A("Fk"), Op.subtract)
        scan(A("s5"), PS(3, 0, 60), A("d5"), 1.0, Op.min, Op.max)
        swap(5, 0, "s5", 6, [("PH", 3), ("PB", 4)])
        swap(2, 0, "s5", 6, [("PH", 2)])
        tt(A("mS"), SA, A("mOld"), Op.min)
        ts(A("fr"), A("s5", 2, 60, 6), 0.25, Op.is_gt, 32768.0, Op.mult)
        tt(A("mOld"), A("mS"), A("fr"), Op.max)
        if t >= 1:
            leavers(t)

    if "seq" not in PLAN:
        PLAN["seq"] = arrange(nodes)
    emit(PLAN["seq"])
